import numpy as np
import ml_dtypes


def mxq(x, axis, fmt="e4m3"):
    dtype, down = {"e4m3": (ml_dtypes.float8_e4m3fn, 7), "e5m2": (ml_dtypes.float8_e5m2, 14)}[fmt]
    v = np.moveaxis(np.asarray(x, np.float32).astype(ml_dtypes.bfloat16).astype(np.float64), axis, -1)
    blocks = v.reshape(v.shape[:-1] + (-1, 32))
    amax = np.abs(blocks).max(-1, keepdims=True)
    byte = np.maximum(np.where(amax > 0, np.frexp(amax)[1] - 1 + 127, 0) - down, 1)
    scale = np.exp2(byte - 127.0)
    codes = (blocks / scale).astype(np.float32).astype(dtype).astype(np.float64)
    return np.moveaxis((codes * scale).reshape(v.shape), -1, axis)


WIDE = False


def mx_kscale(k):
    if not WIDE:
        return np.ones(k)
    levels = np.array([10, -10, 5, -5, 0])
    if k % 512:
        return np.exp2(np.random.permutation(np.resize(levels, k // 32))).repeat(32)
    a = np.empty((k // 512, 16))
    for p in range(k // 512):
        a[p, :8] = np.random.permutation(np.resize(levels, 8))
        for g in range(8):
            far = levels[np.abs(levels - a[p, g]) >= 10]
            a[p, g + 8] = far[np.random.randint(len(far))]
    return np.exp2(a.ravel()).repeat(32)


def f64(x):
    return np.asarray(x).astype(np.float64)


def striped(idx):
    return np.tile(idx.reshape(-1, 16).T, (8, 1)).astype(np.uint16)


def unstriped(offs):
    return offs[:16].T.reshape(-1).astype(np.int64)


def pack_weight(w):
    k, n = w.shape
    w = f64(np.asarray(w, np.float32).astype(ml_dtypes.bfloat16)).reshape(k // 32, 32, n)
    amax = np.abs(w).max(1)
    byte = np.clip(np.where(amax > 0, np.frexp(amax)[1] - 1 + 127 - 7, 1), 1, 254)
    scaled = (w * np.exp2(127.0 - byte)[:, None, :]).reshape(k, n).astype(np.float32)
    words = np.ascontiguousarray(scaled.reshape(k // 512, 128, 4, n).transpose(0, 1, 3, 2)).astype(ml_dtypes.float8_e4m3fn).view(np.uint8)
    return words, np.ascontiguousarray(byte.astype(np.uint8).reshape(k // 512, 16, n))


def unpack_weight(words, scales):
    g, p, n, _ = words.shape
    vals = np.ascontiguousarray(words).view(ml_dtypes.float8_e4m3fn).astype(np.float64) * np.repeat(np.exp2(scales.astype(np.float64) - 127.0), 8, axis=1)[..., None]
    return vals.transpose(0, 1, 3, 2).reshape(g * 512, n)


def relu(v):
    return np.maximum(v, 0.0)


K, T, S, V, H, N = 512, 2048, 512, 256, 512, 256


def setup_inputs():
    n = np.random.standard_normal
    s = mx_kscale(K)[:, None]
    u = mx_kscale(H)
    near = np.random.permutation(S)
    packed_xT = pack_weight(n((K, T)) * s)
    return {
        "x_words": packed_xT[0],
        "x_scales": packed_xT[1],
        "w1": (n((K, H)) / np.sqrt(K) / s * u).astype(np.float32),
        "w2": (n((H, N)) / np.sqrt(H) / u[:, None]).astype(np.float32),
        "offs": striped(np.random.permutation(T)[:S]),
        "pos1": striped(near[:V]),
        "pos2": striped(near[V:]),
        "pos3": striped(np.random.permutation(S)[:V]),
    }


def reference(x_words, x_scales, w1, w2, offs, pos1, pos2, pos3):
    xq = unpack_weight(x_words, x_scales)[:, unstriped(offs)]
    h = mxq(f64(w1), 0, "e4m3").T @ xq
    g0 = h[:, unstriped(pos1)]
    g1 = h[:, unstriped(pos2)]
    g2 = h[:, unstriped(pos3)]
    hi = np.maximum(np.maximum(g0, g1), g2)
    lo = np.minimum(np.minimum(g0, g1), g2)
    z = (g0 + g1 + g2 - hi - lo) / 1
    return relu(mxq(f64(w2), 0, "e4m3").T @ mxq(z, 0, "e4m3"))

@@ -1,0 +1,184 @@
+from contextlib import ExitStack
+
+import concourse.mybir as mybir
+
+K, T, S, V, H, N = 512, 2048, 512, 256, 512, 256
+FLOPS = 2 * K * H * S + 2 * H * N * V
+
+F32 = mybir.dt.float32
+BF16 = mybir.dt.bfloat16
+I32 = mybir.dt.int32
+U32 = mybir.dt.uint32
+U16 = mybir.dt.uint16
+U8 = mybir.dt.uint8
+FP8X4 = mybir.dt.float8_e4m3fn_x4
+ALU = mybir.AluOpType
+ACT = mybir.ActivationFunctionType
+
+P = 128
+PACK = 4
+HALF_S = S // 2
+HALF_V = V // 2
+
+
+def tile_picked_ytrim_relu_p_kernel(
+    tc, x_words, x_scales, w1, w2, offs, pos1, pos2, pos3, out
+):
+    nc = tc.nc
+    with ExitStack() as ctx:
+        lists = ctx.enter_context(tc.tile_pool(name="lists", bufs=1))
+        sb = ctx.enter_context(tc.tile_pool(name="sb", bufs=1))
+        reuse = ctx.enter_context(tc.tile_pool(name="reuse", bufs=1))
+        psum = ctx.enter_context(tc.psum_pool(name="psum", bufs=1))
+
+        offs_sb = lists.tile([P, S // 16], U16, name="offs_sb")
+        pos_sb = [lists.tile([P, V // 16], U16, name="pos_sb%d" % d) for d in range(3)]
+
+        scale_win = reuse.tile([P, T], U8, name="scale_win", align_bytes=64, offset=4 * P)
+        word_win = reuse.tile([P, T], I32, name="word_win", align_bytes=64, offset=2 * T)
+        w1_raw = sb.tile([P, PACK, H], F32, name="w1_raw", tag="w_raw")
+        warm = sb.tile([P, 8], F32, name="warm")
+        warm_out = sb.tile([P, 8], F32, name="warm_out")
+
+        nc.vector.memset(scale_win[:].bitcast(I32), 0)
+        nc.vector.memset(warm[:], 0.0)
+
+        nc.sync.dma_start(offs_sb[:], offs)
+        nc.sync.dma_start(pos_sb[0][:], pos1)
+        nc.sync.dma_start(w1_raw[:], w1.rearrange("(p j) c -> p j c", j=PACK))
+        nc.sync.dma_start(word_win[:], x_words[0].rearrange("p n t -> p (n t)").bitcast(I32))
+        nc.sync.dma_start(pos_sb[1][:], pos2)
+        nc.sync.dma_start(pos_sb[2][:], pos3)
+        for q in range(4):
+            nc.scalar.dma_start(
+                scale_win[32 * q : 32 * q + 4, :].bitcast(I32),
+                x_scales[0, 4 * q : 4 * q + 4, :].bitcast(I32),
+            )
+        nc.scalar.activation(warm_out[:], warm[:], ACT.Relu)
+
+        x_sc = sb.tile([P, S], U8, name="x_sc", align_bytes=64)
+        nc.vector.tensor_copy(x_sc[:], scale_win[:].indirect(offs_sb[:]))
+
+        w1_bf = sb.tile([P, H * PACK], BF16, name="w1_bf", align_bytes=64)
+        w1_dst = w1_bf[:].rearrange("p (t m j) -> p m j t", t=PACK, j=PACK)
+        w1_src = w1_raw[:].rearrange("p j (m t) -> p m j t", t=PACK)
+        nc.scalar.copy(w1_dst[:, 0:64], w1_src[:, 0:64])
+        nc.vector.tensor_copy(w1_dst[:, 64:128], w1_src[:, 64:128])
+        w1_q0 = reuse.tile([P, P], U32, name="w1_q0", align_bytes=64, offset=4 * S)
+        w1_sc = sb.tile([P, H], U8, name="w1_sc", align_bytes=64)
+        nc.vector.quantize_mx(out=w1_q0[:].bitcast(FP8X4), scales=w1_sc[:, 0:P], in_=w1_bf[:, 0 : P * PACK])
+
+        w2_raw = sb.tile([P, PACK, N], F32, name="w2_raw", tag="w_raw")
+        nc.sync.dma_start(w2_raw[:], w2.rearrange("(p j) n -> p j n", j=PACK))
+
+        x_q = reuse.tile([P, S], U32, name="x_q", align_bytes=64, offset=0)
+        for a in range(2):
+            nc.vector.tensor_copy(
+                x_q[:, a * HALF_S : (a + 1) * HALF_S],
+                word_win[:].bitcast(U32).indirect(offs_sb[:, a * 16 : (a + 1) * 16]),
+            )
+
+        w1_q123 = reuse.tile([P, H - P], U32, name="w1_q123", align_bytes=64, offset=2 * T)
+        nc.vector.quantize_mx(out=w1_q123[:, 0:P].bitcast(FP8X4), scales=w1_sc[:, P : 2 * P], in_=w1_bf[:, P * PACK : 2 * P * PACK])
+        nc.vector.quantize_mx(out=w1_q123[:, P:].bitcast(FP8X4), scales=w1_sc[:, 2 * P :], in_=w1_bf[:, 2 * P * PACK :])
+        w1_q = [w1_q0[:]] + [w1_q123[:, t * P : (t + 1) * P] for t in range(PACK - 1)]
+
+        def first_product(acc, t, cols):
+            rows = slice(t * P, (t + 1) * P)
+            nc.tensor.matmul_mx(
+                out=acc, lhsT=w1_q[t].bitcast(FP8X4), lhsT_scale=w1_sc[:, rows],
+                rhs=x_q[:, cols].bitcast(FP8X4), rhs_scale=x_sc[:, cols], start=True, stop=True,
+            )
+
+        h = [sb.tile([P, S], F32, name="h%d" % t) for t in range(PACK)]
+        for a in range(2):
+            cols = slice(a * HALF_S, (a + 1) * HALF_S)
+            acc = psum.tile([P, HALF_S], F32, name="h0_ps%d" % a)
+            first_product(acc[:], 0, cols)
+            nc.scalar.copy(h[0][:, cols], acc[:])
+        for t in range(1, PACK):
+            acc = psum.tile([P, S], F32, name="h_ps%d" % t)
+            first_product(acc[:], t, slice(0, S))
+            nc.scalar.copy(h[t][:], acc[:])
+
+        w2_bf = sb.tile([P, N * PACK], BF16, name="w2_bf", align_bytes=64)
+        nc.scalar.copy(
+            w2_bf[:].rearrange("p (c i j) -> p c j i", i=4, j=PACK),
+            w2_raw[:].rearrange("p j (c i) -> p c j i", i=4),
+        )
+        w2_q = sb.tile([P, N], U32, name="w2_q", align_bytes=64)
+        w2_sc = sb.tile([P, N], U8, name="w2_sc", align_bytes=64)
+
+        g0 = sb.tile([P, PACK, V], F32, name="g0")
+        d1 = sb.tile([P, PACK, V], F32, name="d1")
+        d2 = sb.tile([P, PACK, V], F32, name="d2")
+        upper = sb.tile([P, PACK, V], F32, name="upper")
+        mid = sb.tile([P, PACK, V], F32, name="mid")
+
+        def fetch(t):
+            nc.vector.tensor_copy(g0[:, t, :], h[t][:].indirect(pos_sb[0][:]))
+
+        def diff(dst, d, t):
+            nc.vector.tensor_tensor(dst[:, t, :], h[t][:].indirect(pos_sb[d][:]), g0[:, t, :], ALU.subtract)
+
+        def clip_above(t, cols):
+            nc.vector.scalar_tensor_tensor(upper[:, t, cols], d1[:, t, cols], 0.0, d2[:, t, cols], ALU.max, ALU.min)
+
+        def clip_below(t, cols):
+            nc.vector.scalar_tensor_tensor(mid[:, t, cols], d1[:, t, cols], 0.0, upper[:, t, cols], ALU.min, ALU.max)
+
+        whole = slice(0, V)
+        halves = [slice(a * HALF_V, (a + 1) * HALF_V) for a in range(2)]
+        last = PACK - 1
+        fetch(0)
+        diff(d1, 1, 0)
+        diff(d2, 2, 0)
+        for t in range(1, PACK):
+            fetch(t)
+            clip_above(t - 1, whole)
+            diff(d1, 1, t)
+            if t == last:
+                nc.vector.quantize_mx(out=w2_q[:].bitcast(FP8X4), scales=w2_sc[:], in_=w2_bf[:])
+            diff(d2, 2, t)
+            clip_below(t - 1, whole)
+        for cols in halves:
+            clip_above(last, cols)
+        for cols in halves:
+            clip_below(last, cols)
+
+        z_bf = [sb.tile([P, HALF_V * PACK], BF16, name="z_bf%d" % a, align_bytes=64) for a in range(2)]
+        z_q = [sb.tile([P, HALF_V], U32, name="z_q%d" % a, align_bytes=64) for a in range(2)]
+        z_sc = [sb.tile([P, HALF_V], U8, name="z_sc%d" % a, align_bytes=64) for a in range(2)]
+        for a, cols in enumerate(halves):
+            nc.vector.tensor_tensor(
+                z_bf[a][:].rearrange("p (c i t) -> p c t i", i=4, t=PACK),
+                mid[:, :, cols].rearrange("p t (c i) -> p c t i", i=4),
+                g0[:, :, cols].rearrange("p t (c i) -> p c t i", i=4),
+                ALU.add,
+            )
+        for a in range(2):
+            nc.vector.quantize_mx(out=z_q[a][:].bitcast(FP8X4), scales=z_sc[a][:], in_=z_bf[a][:])
+
+        def second_product(acc, a, b):
+            rows = slice(b * P, (b + 1) * P)
+            nc.tensor.matmul_mx(
+                out=acc, lhsT=w2_q[:, rows].bitcast(FP8X4), lhsT_scale=w2_sc[:, rows],
+                rhs=z_q[a][:].bitcast(FP8X4), rhs_scale=z_sc[a][:], start=True, stop=True,
+            )
+
+        acc0 = psum.tile([P, 2, HALF_V], F32, name="o_ps0")
+        res0 = sb.tile([P, 2, HALF_V], F32, name="res0")
+        for b in range(2):
+            second_product(acc0[:, b, :], 0, b)
+        nc.scalar.activation(res0[:], acc0[:], ACT.Relu)
+        nc.sync.dma_start(out[:, halves[0]].rearrange("(b p) v -> p b v", p=P), res0[:])
+        for b in range(2):
+            acc1 = psum.tile([P, HALF_V], F32, name="o_ps1%d" % b)
+            res1 = sb.tile([P, HALF_V], F32, name="res1%d" % b)
+            second_product(acc1[:], 1, b)
+            if b == 0:
+                nc.vector.tensor_scalar_max(res1[:], acc1[:], 0.0)
+                nc.sync.dma_start(out[0:P, halves[1]], res1[:])
+            else:
+                nc.scalar.activation(res1[:], acc1[:], ACT.Relu)
+                nc.scalar.dma_start(out[P:N, halves[1]], res1[:])

@@ -37,24 +37,21 @@ def tile_picked_ytrim_relu_p_kernel(
         scale_win = reuse.tile([P, T], U8, name="scale_win", align_bytes=64, offset=4 * P)
         word_win = reuse.tile([P, T], I32, name="word_win", align_bytes=64, offset=2 * T)
         w1_raw = sb.tile([P, PACK, H], F32, name="w1_raw", tag="w_raw")
-        warm = sb.tile([P, 8], F32, name="warm")
-        warm_out = sb.tile([P, 8], F32, name="warm_out")
 
-        nc.vector.memset(scale_win[:].bitcast(I32), 0)
-        nc.vector.memset(warm[:], 0.0)
+        nc.gpsimd.memset(scale_win[:].bitcast(I32)[:, 0:256], 0)
+        nc.vector.memset(scale_win[:].bitcast(I32)[:, 256:512], 0)
 
         nc.sync.dma_start(offs_sb[:], offs)
-        nc.sync.dma_start(pos_sb[0][:], pos1)
         nc.sync.dma_start(w1_raw[:], w1.rearrange("(p j) c -> p j c", j=PACK))
-        nc.sync.dma_start(word_win[:], x_words[0].rearrange("p n t -> p (n t)").bitcast(I32))
-        nc.sync.dma_start(pos_sb[1][:], pos2)
-        nc.sync.dma_start(pos_sb[2][:], pos3)
         for q in range(4):
-            nc.scalar.dma_start(
+            nc.sync.dma_start(
                 scale_win[32 * q : 32 * q + 4, :].bitcast(I32),
                 x_scales[0, 4 * q : 4 * q + 4, :].bitcast(I32),
             )
-        nc.scalar.activation(warm_out[:], warm[:], ACT.Relu)
+        nc.sync.dma_start(pos_sb[0][:], pos1)
+        nc.sync.dma_start(word_win[:], x_words[0].rearrange("p n t -> p (n t)").bitcast(I32))
+        nc.sync.dma_start(pos_sb[1][:], pos2)
+        nc.sync.dma_start(pos_sb[2][:], pos3)
 
         x_sc = sb.tile([P, S], U8, name="x_sc", align_bytes=64)
         nc.vector.tensor_copy(x_sc[:], scale_win[:].indirect(offs_sb[:]))
@@ -62,8 +59,8 @@ def tile_picked_ytrim_relu_p_kernel(
         w1_bf = sb.tile([P, H * PACK], BF16, name="w1_bf", align_bytes=64)
         w1_dst = w1_bf[:].rearrange("p (t m j) -> p m j t", t=PACK, j=PACK)
         w1_src = w1_raw[:].rearrange("p j (m t) -> p m j t", t=PACK)
-        nc.scalar.copy(w1_dst[:, 0:64], w1_src[:, 0:64])
-        nc.vector.tensor_copy(w1_dst[:, 64:128], w1_src[:, 64:128])
+        nc.scalar.copy(w1_dst[:, 0:80], w1_src[:, 0:80])
+        nc.vector.tensor_copy(w1_dst[:, 80:128], w1_src[:, 80:128])
         w1_q0 = reuse.tile([P, P], U32, name="w1_q0", align_bytes=64, offset=4 * S)
         w1_sc = sb.tile([P, H], U8, name="w1_sc", align_bytes=64)
         nc.vector.quantize_mx(out=w1_q0[:].bitcast(FP8X4), scales=w1_sc[:, 0:P], in_=w1_bf[:, 0 : P * PACK])
@@ -71,10 +68,10 @@ def tile_picked_ytrim_relu_p_kernel(
         w2_raw = sb.tile([P, PACK, N], F32, name="w2_raw", tag="w_raw")
         nc.sync.dma_start(w2_raw[:], w2.rearrange("(p j) n -> p j n", j=PACK))
 
-        x_q = reuse.tile([P, S], U32, name="x_q", align_bytes=64, offset=0)
+        x_q = [reuse.tile([P, HALF_S], U32, name="x_q%d" % a, align_bytes=64, offset=4 * HALF_S * a) for a in range(2)]
         for a in range(2):
             nc.vector.tensor_copy(
-                x_q[:, a * HALF_S : (a + 1) * HALF_S],
+                x_q[a][:],
                 word_win[:].bitcast(U32).indirect(offs_sb[:, a * 16 : (a + 1) * 16]),
             )
 
@@ -83,23 +80,29 @@ def tile_picked_ytrim_relu_p_kernel(
         nc.vector.quantize_mx(out=w1_q123[:, P:].bitcast(FP8X4), scales=w1_sc[:, 2 * P :], in_=w1_bf[:, 2 * P * PACK :])
         w1_q = [w1_q0[:]] + [w1_q123[:, t * P : (t + 1) * P] for t in range(PACK - 1)]
 
-        def first_product(acc, t, cols):
+        def first_product(acc, t, a, c0, c1):
             rows = slice(t * P, (t + 1) * P)
             nc.tensor.matmul_mx(
                 out=acc, lhsT=w1_q[t].bitcast(FP8X4), lhsT_scale=w1_sc[:, rows],
-                rhs=x_q[:, cols].bitcast(FP8X4), rhs_scale=x_sc[:, cols], start=True, stop=True,
+                rhs=x_q[a][:, c0:c1].bitcast(FP8X4), rhs_scale=x_sc[:, a * HALF_S + c0 : a * HALF_S + c1],
+                start=True, stop=True,
             )
 
         h = [sb.tile([P, S], F32, name="h%d" % t) for t in range(PACK)]
-        for a in range(2):
-            cols = slice(a * HALF_S, (a + 1) * HALF_S)
-            acc = psum.tile([P, HALF_S], F32, name="h0_ps%d" % a)
-            first_product(acc[:], 0, cols)
-            nc.scalar.copy(h[0][:, cols], acc[:])
+        acc = psum.tile([P, HALF_S], F32, name="h0_ps0", tag="first")
+        first_product(acc[:], 0, 0, 0, HALF_S)
+        nc.scalar.copy(h[0][:, 0:HALF_S], acc[:])
+        acc = psum.tile([P, P], F32, name="h0_ps1")
+        first_product(acc[:], 0, 1, 0, P)
+        nc.scalar.copy(h[0][:, HALF_S : HALF_S + P], acc[:])
+        acc = psum.tile([P, P], F32, name="h0_ps2")
+        first_product(acc[:], 0, 1, P, HALF_S)
+        nc.vector.tensor_copy(h[0][:, HALF_S + P :], acc[:])
         for t in range(1, PACK):
-            acc = psum.tile([P, S], F32, name="h_ps%d" % t)
-            first_product(acc[:], t, slice(0, S))
-            nc.scalar.copy(h[t][:], acc[:])
+            acc = psum.tile([P, 2, HALF_S], F32, name="h_ps%d" % t)
+            for a in range(2):
+                first_product(acc[:, a, :], t, a, 0, HALF_S)
+            nc.scalar.copy(h[t][:], acc[:].rearrange("p a c -> p (a c)"))
 
         w2_bf = sb.tile([P, N * PACK], BF16, name="w2_bf", align_bytes=64)
         nc.scalar.copy(
@@ -109,42 +112,19 @@ def tile_picked_ytrim_relu_p_kernel(
         w2_q = sb.tile([P, N], U32, name="w2_q", align_bytes=64)
         w2_sc = sb.tile([P, N], U8, name="w2_sc", align_bytes=64)
 
-        g0 = sb.tile([P, PACK, V], F32, name="g0")
-        d1 = sb.tile([P, PACK, V], F32, name="d1")
-        d2 = sb.tile([P, PACK, V], F32, name="d2")
-        upper = sb.tile([P, PACK, V], F32, name="upper")
-        mid = sb.tile([P, PACK, V], F32, name="mid")
-
-        def fetch(t):
-            nc.vector.tensor_copy(g0[:, t, :], h[t][:].indirect(pos_sb[0][:]))
-
-        def diff(dst, d, t):
-            nc.vector.tensor_tensor(dst[:, t, :], h[t][:].indirect(pos_sb[d][:]), g0[:, t, :], ALU.subtract)
-
-        def clip_above(t, cols):
-            nc.vector.scalar_tensor_tensor(upper[:, t, cols], d1[:, t, cols], 0.0, d2[:, t, cols], ALU.max, ALU.min)
-
-        def clip_below(t, cols):
-            nc.vector.scalar_tensor_tensor(mid[:, t, cols], d1[:, t, cols], 0.0, upper[:, t, cols], ALU.min, ALU.max)
-
-        whole = slice(0, V)
+        g = [sb.tile([P, PACK, V], BF16, name="g%d" % d, align_bytes=64) for d in range(3)]
+        hi = sb.tile([P, PACK, V], BF16, name="hi", align_bytes=64)
+        lo = sb.tile([P, PACK, V], BF16, name="lo", align_bytes=64)
+        capped = sb.tile([P, PACK, V], BF16, name="capped", align_bytes=64)
         halves = [slice(a * HALF_V, (a + 1) * HALF_V) for a in range(2)]
-        last = PACK - 1
-        fetch(0)
-        diff(d1, 1, 0)
-        diff(d2, 2, 0)
-        for t in range(1, PACK):
-            fetch(t)
-            clip_above(t - 1, whole)
-            diff(d1, 1, t)
-            if t == last:
-                nc.vector.quantize_mx(out=w2_q[:].bitcast(FP8X4), scales=w2_sc[:], in_=w2_bf[:])
-            diff(d2, 2, t)
-            clip_below(t - 1, whole)
+        for t in range(PACK):
+            for d in range(3):
+                nc.vector.tensor_copy(g[d][:, t, :], h[t][:].indirect(pos_sb[d][:]))
+        nc.vector.quantize_mx(out=w2_q[:].bitcast(FP8X4), scales=w2_sc[:], in_=w2_bf[:])
+        nc.vector.tensor_tensor(hi[:], g[0][:], g[1][:], ALU.max)
+        nc.vector.tensor_tensor(lo[:], g[0][:], g[1][:], ALU.min)
         for cols in halves:
-            clip_above(last, cols)
-        for cols in halves:
-            clip_below(last, cols)
+            nc.vector.tensor_tensor(capped[:, :, cols], hi[:, :, cols], g[2][:, :, cols], ALU.min)
 
         z_bf = [sb.tile([P, HALF_V * PACK], BF16, name="z_bf%d" % a, align_bytes=64) for a in range(2)]
         z_q = [sb.tile([P, HALF_V], U32, name="z_q%d" % a, align_bytes=64) for a in range(2)]
@@ -152,9 +132,9 @@ def tile_picked_ytrim_relu_p_kernel(
         for a, cols in enumerate(halves):
             nc.vector.tensor_tensor(
                 z_bf[a][:].rearrange("p (c i t) -> p c t i", i=4, t=PACK),
-                mid[:, :, cols].rearrange("p t (c i) -> p c t i", i=4),
-                g0[:, :, cols].rearrange("p t (c i) -> p c t i", i=4),
-                ALU.add,
+                capped[:, :, cols].rearrange("p t (c i) -> p c t i", i=4),
+                lo[:, :, cols].rearrange("p t (c i) -> p c t i", i=4),
+                ALU.max,
             )
         for a in range(2):
             nc.vector.quantize_mx(out=z_q[a][:].bitcast(FP8X4), scales=z_sc[a][:], in_=z_bf[a][:])
@@ -166,7 +146,7 @@ def tile_picked_ytrim_relu_p_kernel(
                 rhs=z_q[a][:].bitcast(FP8X4), rhs_scale=z_sc[a][:], start=True, stop=True,
             )
 
-        acc0 = psum.tile([P, 2, HALF_V], F32, name="o_ps0")
+        acc0 = psum.tile([P, 2, HALF_V], F32, name="o_ps0", tag="first")
         res0 = sb.tile([P, 2, HALF_V], F32, name="res0")
         for b in range(2):
             second_product(acc0[:, b, :], 0, b)

@@ -28,18 +28,17 @@ def tile_picked_ytrim_relu_p_kernel(
     with ExitStack() as ctx:
         lists = ctx.enter_context(tc.tile_pool(name="lists", bufs=1))
         sb = ctx.enter_context(tc.tile_pool(name="sb", bufs=1))
-        reuse = ctx.enter_context(tc.tile_pool(name="reuse", bufs=1))
         psum = ctx.enter_context(tc.psum_pool(name="psum", bufs=1))
 
         offs_sb = lists.tile([P, S // 16], U16, name="offs_sb")
         pos_sb = [lists.tile([P, V // 16], U16, name="pos_sb%d" % d) for d in range(3)]
 
-        scale_win = reuse.tile([P, T], U8, name="scale_win", align_bytes=64, offset=4 * P)
-        word_win = reuse.tile([P, T], I32, name="word_win", align_bytes=64, offset=2 * T)
-        w1_raw = sb.tile([P, PACK, H], F32, name="w1_raw", tag="w_raw")
+        scale_win = sb.tile([P, T], U8, name="scale_win", align_bytes=64)
+        word_win = sb.tile([P, T], I32, name="word_win", align_bytes=64)
+        w1_raw = sb.tile([P, PACK, H], F32, name="w1_raw")
 
-        nc.gpsimd.memset(scale_win[:].bitcast(I32)[:, 0:256], 0)
-        nc.vector.memset(scale_win[:].bitcast(I32)[:, 256:512], 0)
+        nc.gpsimd.memset(scale_win[:].bitcast(I32)[:, 0:128], 0)
+        nc.vector.memset(scale_win[:].bitcast(I32)[:, 128:512], 0)
 
         nc.sync.dma_start(offs_sb[:], offs)
         nc.sync.dma_start(w1_raw[:], w1.rearrange("(p j) c -> p j c", j=PACK))
@@ -50,6 +49,8 @@ def tile_picked_ytrim_relu_p_kernel(
             )
         nc.sync.dma_start(pos_sb[0][:], pos1)
         nc.sync.dma_start(word_win[:], x_words[0].rearrange("p n t -> p (n t)").bitcast(I32))
+        w2_raw = sb.tile([P, PACK, N], F32, name="w2_raw")
+        nc.sync.dma_start(w2_raw[:], w2.rearrange("(p j) n -> p j n", j=PACK))
         nc.sync.dma_start(pos_sb[1][:], pos2)
         nc.sync.dma_start(pos_sb[2][:], pos3)
 
@@ -59,31 +60,32 @@ def tile_picked_ytrim_relu_p_kernel(
         w1_bf = sb.tile([P, H * PACK], BF16, name="w1_bf", align_bytes=64)
         w1_dst = w1_bf[:].rearrange("p (t m j) -> p m j t", t=PACK, j=PACK)
         w1_src = w1_raw[:].rearrange("p j (m t) -> p m j t", t=PACK)
-        nc.scalar.copy(w1_dst[:, 0:80], w1_src[:, 0:80])
-        nc.vector.tensor_copy(w1_dst[:, 80:128], w1_src[:, 80:128])
-        w1_q0 = reuse.tile([P, P], U32, name="w1_q0", align_bytes=64, offset=4 * S)
+        nc.scalar.copy(w1_dst[:, 0:72], w1_src[:, 0:72])
+        nc.vector.tensor_copy(w1_dst[:, 72:128], w1_src[:, 72:128])
+        w1_q = sb.tile([P, H], U32, name="w1_q", align_bytes=64)
         w1_sc = sb.tile([P, H], U8, name="w1_sc", align_bytes=64)
-        nc.vector.quantize_mx(out=w1_q0[:].bitcast(FP8X4), scales=w1_sc[:, 0:P], in_=w1_bf[:, 0 : P * PACK])
+        nc.vector.quantize_mx(out=w1_q[:].bitcast(FP8X4), scales=w1_sc[:], in_=w1_bf[:])
 
-        w2_raw = sb.tile([P, PACK, N], F32, name="w2_raw", tag="w_raw")
-        nc.sync.dma_start(w2_raw[:], w2.rearrange("(p j) n -> p j n", j=PACK))
-
-        x_q = [reuse.tile([P, HALF_S], U32, name="x_q%d" % a, align_bytes=64, offset=4 * HALF_S * a) for a in range(2)]
+        x_q = [sb.tile([P, HALF_S], U32, name="x_q%d" % a, align_bytes=64) for a in range(2)]
         for a in range(2):
             nc.vector.tensor_copy(
                 x_q[a][:],
                 word_win[:].bitcast(U32).indirect(offs_sb[:, a * 16 : (a + 1) * 16]),
             )
 
-        w1_q123 = reuse.tile([P, H - P], U32, name="w1_q123", align_bytes=64, offset=2 * T)
-        nc.vector.quantize_mx(out=w1_q123[:, 0:P].bitcast(FP8X4), scales=w1_sc[:, P : 2 * P], in_=w1_bf[:, P * PACK : 2 * P * PACK])
-        nc.vector.quantize_mx(out=w1_q123[:, P:].bitcast(FP8X4), scales=w1_sc[:, 2 * P :], in_=w1_bf[:, 2 * P * PACK :])
-        w1_q = [w1_q0[:]] + [w1_q123[:, t * P : (t + 1) * P] for t in range(PACK - 1)]
+        w2_bf = sb.tile([P, N * PACK], BF16, name="w2_bf", align_bytes=64)
+        nc.vector.tensor_copy(
+            w2_bf[:].rearrange("p (c i j) -> p c j i", i=4, j=PACK),
+            w2_raw[:].rearrange("p j (c i) -> p c j i", i=4),
+        )
+        w2_q = sb.tile([P, N], U32, name="w2_q", align_bytes=64)
+        w2_sc = sb.tile([P, N], U8, name="w2_sc", align_bytes=64)
+        nc.vector.quantize_mx(out=w2_q[:].bitcast(FP8X4), scales=w2_sc[:], in_=w2_bf[:])
 
         def first_product(acc, t, a, c0, c1):
             rows = slice(t * P, (t + 1) * P)
             nc.tensor.matmul_mx(
-                out=acc, lhsT=w1_q[t].bitcast(FP8X4), lhsT_scale=w1_sc[:, rows],
+                out=acc, lhsT=w1_q[:, rows].bitcast(FP8X4), lhsT_scale=w1_sc[:, rows],
                 rhs=x_q[a][:, c0:c1].bitcast(FP8X4), rhs_scale=x_sc[:, a * HALF_S + c0 : a * HALF_S + c1],
                 start=True, stop=True,
             )
@@ -97,20 +99,12 @@ def tile_picked_ytrim_relu_p_kernel(
         nc.scalar.copy(h[0][:, HALF_S : HALF_S + P], acc[:])
         acc = psum.tile([P, P], F32, name="h0_ps2")
         first_product(acc[:], 0, 1, P, HALF_S)
-        nc.vector.tensor_copy(h[0][:, HALF_S + P :], acc[:])
+        nc.scalar.copy(h[0][:, HALF_S + P :], acc[:])
         for t in range(1, PACK):
             acc = psum.tile([P, 2, HALF_S], F32, name="h_ps%d" % t)
             for a in range(2):
                 first_product(acc[:, a, :], t, a, 0, HALF_S)
             nc.scalar.copy(h[t][:], acc[:].rearrange("p a c -> p (a c)"))
-
-        w2_bf = sb.tile([P, N * PACK], BF16, name="w2_bf", align_bytes=64)
-        nc.scalar.copy(
-            w2_bf[:].rearrange("p (c i j) -> p c j i", i=4, j=PACK),
-            w2_raw[:].rearrange("p j (c i) -> p c j i", i=4),
-        )
-        w2_q = sb.tile([P, N], U32, name="w2_q", align_bytes=64)
-        w2_sc = sb.tile([P, N], U8, name="w2_sc", align_bytes=64)
 
         g = [sb.tile([P, PACK, V], BF16, name="g%d" % d, align_bytes=64) for d in range(3)]
         hi = sb.tile([P, PACK, V], BF16, name="hi", align_bytes=64)
@@ -120,7 +114,6 @@ def tile_picked_ytrim_relu_p_kernel(
         for t in range(PACK):
             for d in range(3):
                 nc.vector.tensor_copy(g[d][:, t, :], h[t][:].indirect(pos_sb[d][:]))
-        nc.vector.quantize_mx(out=w2_q[:].bitcast(FP8X4), scales=w2_sc[:], in_=w2_bf[:])
         nc.vector.tensor_tensor(hi[:], g[0][:], g[1][:], ALU.max)
         nc.vector.tensor_tensor(lo[:], g[0][:], g[1][:], ALU.min)
         for cols in halves:

@@ -17,8 +17,15 @@ ACT = mybir.ActivationFunctionType
 
 P = 128
 PACK = 4
+LIST_ROWS = 16
+QUADRANT = 32
 HALF_S = S // 2
 HALF_V = V // 2
+QUARTER_V = V // 4
+RUN = 4
+ALIGN = 64
+GPSIMD_CLEARS = 128
+SCALAR_DEALS = 72
 
 
 def tile_picked_ytrim_relu_p_kernel(
@@ -30,21 +37,21 @@ def tile_picked_ytrim_relu_p_kernel(
         sb = ctx.enter_context(tc.tile_pool(name="sb", bufs=1))
         psum = ctx.enter_context(tc.psum_pool(name="psum", bufs=1))
 
-        offs_sb = lists.tile([P, S // 16], U16, name="offs_sb")
-        pos_sb = [lists.tile([P, V // 16], U16, name="pos_sb%d" % d) for d in range(3)]
+        offs_sb = lists.tile([P, S // LIST_ROWS], U16, name="offs_sb")
+        pos_sb = [lists.tile([P, V // LIST_ROWS], U16, name="pos_sb%d" % d) for d in range(3)]
 
-        scale_win = sb.tile([P, T], U8, name="scale_win", align_bytes=64)
-        word_win = sb.tile([P, T], I32, name="word_win", align_bytes=64)
+        scale_win = sb.tile([P, T], U8, name="scale_win", align_bytes=ALIGN)
+        word_win = sb.tile([P, T], I32, name="word_win", align_bytes=ALIGN)
         w1_raw = sb.tile([P, PACK, H], F32, name="w1_raw")
 
-        nc.gpsimd.memset(scale_win[:].bitcast(I32)[:, 0:128], 0)
-        nc.vector.memset(scale_win[:].bitcast(I32)[:, 128:512], 0)
+        nc.gpsimd.memset(scale_win[:].bitcast(I32)[:, 0:GPSIMD_CLEARS], 0)
+        nc.vector.memset(scale_win[:].bitcast(I32)[:, GPSIMD_CLEARS : T // 4], 0)
 
         nc.sync.dma_start(offs_sb[:], offs)
         nc.sync.dma_start(w1_raw[:], w1.rearrange("(p j) c -> p j c", j=PACK))
-        for q in range(4):
+        for q in range(P // QUADRANT):
             nc.sync.dma_start(
-                scale_win[32 * q : 32 * q + 4, :].bitcast(I32),
+                scale_win[QUADRANT * q : QUADRANT * q + 4, :].bitcast(I32),
                 x_scales[0, 4 * q : 4 * q + 4, :].bitcast(I32),
             )
         nc.sync.dma_start(pos_sb[0][:], pos1)
@@ -54,104 +61,125 @@ def tile_picked_ytrim_relu_p_kernel(
         nc.sync.dma_start(pos_sb[1][:], pos2)
         nc.sync.dma_start(pos_sb[2][:], pos3)
 
-        x_sc = sb.tile([P, S], U8, name="x_sc", align_bytes=64)
+        x_sc = sb.tile([P, S], U8, name="x_sc", align_bytes=ALIGN)
         nc.vector.tensor_copy(x_sc[:], scale_win[:].indirect(offs_sb[:]))
 
-        w1_bf = sb.tile([P, H * PACK], BF16, name="w1_bf", align_bytes=64)
+        w1_bf = sb.tile([P, H * PACK], BF16, name="w1_bf", align_bytes=ALIGN)
         w1_dst = w1_bf[:].rearrange("p (t m j) -> p m j t", t=PACK, j=PACK)
         w1_src = w1_raw[:].rearrange("p j (m t) -> p m j t", t=PACK)
-        nc.scalar.copy(w1_dst[:, 0:72], w1_src[:, 0:72])
-        nc.vector.tensor_copy(w1_dst[:, 72:128], w1_src[:, 72:128])
-        w1_q = sb.tile([P, H], U32, name="w1_q", align_bytes=64)
-        w1_sc = sb.tile([P, H], U8, name="w1_sc", align_bytes=64)
+        nc.scalar.copy(w1_dst[:, 0:SCALAR_DEALS], w1_src[:, 0:SCALAR_DEALS])
+        nc.vector.tensor_copy(w1_dst[:, SCALAR_DEALS:P], w1_src[:, SCALAR_DEALS:P])
+        w1_q = sb.tile([P, H], U32, name="w1_q", align_bytes=ALIGN)
+        w1_sc = sb.tile([P, H], U8, name="w1_sc", align_bytes=ALIGN)
         nc.vector.quantize_mx(out=w1_q[:].bitcast(FP8X4), scales=w1_sc[:], in_=w1_bf[:])
 
-        x_q = [sb.tile([P, HALF_S], U32, name="x_q%d" % a, align_bytes=64) for a in range(2)]
+        x_q = [sb.tile([P, HALF_S], U32, name="x_q%d" % a, align_bytes=ALIGN) for a in range(2)]
+        list_cols = HALF_S // LIST_ROWS
         for a in range(2):
             nc.vector.tensor_copy(
                 x_q[a][:],
-                word_win[:].bitcast(U32).indirect(offs_sb[:, a * 16 : (a + 1) * 16]),
+                word_win[:].bitcast(U32).indirect(offs_sb[:, a * list_cols : (a + 1) * list_cols]),
             )
 
-        w2_bf = sb.tile([P, N * PACK], BF16, name="w2_bf", align_bytes=64)
+        w2_bf = sb.tile([P, N * PACK], BF16, name="w2_bf", align_bytes=ALIGN)
         nc.vector.tensor_copy(
-            w2_bf[:].rearrange("p (c i j) -> p c j i", i=4, j=PACK),
-            w2_raw[:].rearrange("p j (c i) -> p c j i", i=4),
+            w2_bf[:].rearrange("p (c r j) -> p c j r", r=RUN, j=PACK),
+            w2_raw[:].rearrange("p j (c r) -> p c j r", r=RUN),
         )
-        w2_q = sb.tile([P, N], U32, name="w2_q", align_bytes=64)
-        w2_sc = sb.tile([P, N], U8, name="w2_sc", align_bytes=64)
+        w2_q = sb.tile([P, N], U32, name="w2_q", align_bytes=ALIGN)
+        w2_sc = sb.tile([P, N], U8, name="w2_sc", align_bytes=ALIGN)
         nc.vector.quantize_mx(out=w2_q[:].bitcast(FP8X4), scales=w2_sc[:], in_=w2_bf[:])
 
         def first_product(acc, t, a, c0, c1):
-            rows = slice(t * P, (t + 1) * P)
+            group = slice(t * P, (t + 1) * P)
             nc.tensor.matmul_mx(
-                out=acc, lhsT=w1_q[:, rows].bitcast(FP8X4), lhsT_scale=w1_sc[:, rows],
+                out=acc, lhsT=w1_q[:, group].bitcast(FP8X4), lhsT_scale=w1_sc[:, group],
                 rhs=x_q[a][:, c0:c1].bitcast(FP8X4), rhs_scale=x_sc[:, a * HALF_S + c0 : a * HALF_S + c1],
                 start=True, stop=True,
             )
 
         h = [sb.tile([P, S], F32, name="h%d" % t) for t in range(PACK)]
-        acc = psum.tile([P, HALF_S], F32, name="h0_ps0", tag="first")
-        first_product(acc[:], 0, 0, 0, HALF_S)
-        nc.scalar.copy(h[0][:, 0:HALF_S], acc[:])
-        acc = psum.tile([P, P], F32, name="h0_ps1")
-        first_product(acc[:], 0, 1, 0, P)
-        nc.scalar.copy(h[0][:, HALF_S : HALF_S + P], acc[:])
-        acc = psum.tile([P, P], F32, name="h0_ps2")
-        first_product(acc[:], 0, 1, P, HALF_S)
-        nc.scalar.copy(h[0][:, HALF_S + P :], acc[:])
+        h0_first = psum.tile([P, HALF_S], F32, name="h0_first", tag="reused_bank")
+        first_product(h0_first[:], 0, 0, 0, HALF_S)
+        nc.scalar.copy(h[0][:, 0:HALF_S], h0_first[:])
+        h0_second = psum.tile([P, P], F32, name="h0_second")
+        first_product(h0_second[:], 0, 1, 0, P)
+        nc.scalar.copy(h[0][:, HALF_S : HALF_S + P], h0_second[:])
+        h0_third = psum.tile([P, P], F32, name="h0_third")
+        first_product(h0_third[:], 0, 1, P, HALF_S)
+        nc.scalar.copy(h[0][:, HALF_S + P :], h0_third[:])
         for t in range(1, PACK):
-            acc = psum.tile([P, 2, HALF_S], F32, name="h_ps%d" % t)
+            h_bank = psum.tile([P, 2, HALF_S], F32, name="h_bank%d" % t)
             for a in range(2):
-                first_product(acc[:, a, :], t, a, 0, HALF_S)
-            nc.scalar.copy(h[t][:], acc[:].rearrange("p a c -> p (a c)"))
+                first_product(h_bank[:, a, :], t, a, 0, HALF_S)
+            nc.scalar.copy(h[t][:], h_bank[:].rearrange("p a c -> p (a c)"))
 
-        g = [sb.tile([P, PACK, V], BF16, name="g%d" % d, align_bytes=64) for d in range(3)]
-        hi = sb.tile([P, PACK, V], BF16, name="hi", align_bytes=64)
-        lo = sb.tile([P, PACK, V], BF16, name="lo", align_bytes=64)
-        capped = sb.tile([P, PACK, V], BF16, name="capped", align_bytes=64)
-        halves = [slice(a * HALF_V, (a + 1) * HALF_V) for a in range(2)]
+        g = [sb.tile([P, PACK, V], BF16, name="g%d" % d, align_bytes=ALIGN) for d in range(3)]
+        hi = sb.tile([P, PACK, V], BF16, name="hi", align_bytes=ALIGN)
+        lo = sb.tile([P, PACK, V], BF16, name="lo", align_bytes=ALIGN)
+        capped = sb.tile([P, PACK, V], BF16, name="capped", align_bytes=ALIGN)
+        halves = [slice(u * HALF_V, (u + 1) * HALF_V) for u in range(2)]
         for t in range(PACK):
             for d in range(3):
                 nc.vector.tensor_copy(g[d][:, t, :], h[t][:].indirect(pos_sb[d][:]))
-        nc.vector.tensor_tensor(hi[:], g[0][:], g[1][:], ALU.max)
-        nc.vector.tensor_tensor(lo[:], g[0][:], g[1][:], ALU.min)
-        for cols in halves:
-            nc.vector.tensor_tensor(capped[:, :, cols], hi[:, :, cols], g[2][:, :, cols], ALU.min)
 
-        z_bf = [sb.tile([P, HALF_V * PACK], BF16, name="z_bf%d" % a, align_bytes=64) for a in range(2)]
-        z_q = [sb.tile([P, HALF_V], U32, name="z_q%d" % a, align_bytes=64) for a in range(2)]
-        z_sc = [sb.tile([P, HALF_V], U8, name="z_sc%d" % a, align_bytes=64) for a in range(2)]
-        for a, cols in enumerate(halves):
+        z_bf = [sb.tile([P, HALF_V * PACK], BF16, name="z_bf%d" % u, align_bytes=ALIGN) for u in range(2)]
+        z_q = [sb.tile([P, HALF_V], U32, name="z_q%d" % u, align_bytes=ALIGN) for u in range(2)]
+        z_sc = [sb.tile([P, HALF_V], U8, name="z_sc%d" % u, align_bytes=ALIGN) for u in range(2)]
+
+        def lower(u):
+            nc.vector.tensor_tensor(lo[:, :, halves[u]], g[0][:, :, halves[u]], g[1][:, :, halves[u]], ALU.min)
+
+        def cap(u):
+            nc.vector.tensor_tensor(capped[:, :, halves[u]], hi[:, :, halves[u]], g[2][:, :, halves[u]], ALU.min)
+
+        def median(u, v0, v1):
+            cols = slice(u * HALF_V + v0, u * HALF_V + v1)
             nc.vector.tensor_tensor(
-                z_bf[a][:].rearrange("p (c i t) -> p c t i", i=4, t=PACK),
-                capped[:, :, cols].rearrange("p t (c i) -> p c t i", i=4),
-                lo[:, :, cols].rearrange("p t (c i) -> p c t i", i=4),
+                z_bf[u][:, v0 * PACK : v1 * PACK].rearrange("p (c r t) -> p c t r", r=RUN, t=PACK),
+                capped[:, :, cols].rearrange("p t (c r) -> p c t r", r=RUN),
+                lo[:, :, cols].rearrange("p t (c r) -> p c t r", r=RUN),
                 ALU.max,
             )
-        for a in range(2):
-            nc.vector.quantize_mx(out=z_q[a][:].bitcast(FP8X4), scales=z_sc[a][:], in_=z_bf[a][:])
 
-        def second_product(acc, a, b):
-            rows = slice(b * P, (b + 1) * P)
-            nc.tensor.matmul_mx(
-                out=acc, lhsT=w2_q[:, rows].bitcast(FP8X4), lhsT_scale=w2_sc[:, rows],
-                rhs=z_q[a][:].bitcast(FP8X4), rhs_scale=z_sc[a][:], start=True, stop=True,
+        def quantise(u, v0, v1):
+            nc.vector.quantize_mx(
+                out=z_q[u][:, v0:v1].bitcast(FP8X4), scales=z_sc[u][:, v0:v1], in_=z_bf[u][:, v0 * PACK : v1 * PACK]
             )
 
-        acc0 = psum.tile([P, 2, HALF_V], F32, name="o_ps0", tag="first")
-        res0 = sb.tile([P, 2, HALF_V], F32, name="res0")
+        nc.vector.tensor_tensor(hi[:], g[0][:], g[1][:], ALU.max)
+        lower(0)
+        cap(0)
+        lower(1)
+        median(0, 0, HALF_V)
+        cap(1)
+        quantise(0, 0, HALF_V)
+        median(1, 0, QUARTER_V)
+        median(1, QUARTER_V, HALF_V)
+        quantise(1, 0, QUARTER_V)
+        quantise(1, QUARTER_V, HALF_V)
+
+        def second_product(acc, u, b):
+            features = slice(b * P, (b + 1) * P)
+            nc.tensor.matmul_mx(
+                out=acc, lhsT=w2_q[:, features].bitcast(FP8X4), lhsT_scale=w2_sc[:, features],
+                rhs=z_q[u][:].bitcast(FP8X4), rhs_scale=z_sc[u][:], start=True, stop=True,
+            )
+
+        out_first = psum.tile([P, 2, HALF_V], F32, name="out_first", tag="reused_bank")
+        res_first = sb.tile([P, 2, HALF_V], F32, name="res_first")
         for b in range(2):
-            second_product(acc0[:, b, :], 0, b)
-        nc.scalar.activation(res0[:], acc0[:], ACT.Relu)
-        nc.sync.dma_start(out[:, halves[0]].rearrange("(b p) v -> p b v", p=P), res0[:])
-        for b in range(2):
-            acc1 = psum.tile([P, HALF_V], F32, name="o_ps1%d" % b)
-            res1 = sb.tile([P, HALF_V], F32, name="res1%d" % b)
-            second_product(acc1[:], 1, b)
-            if b == 0:
-                nc.vector.tensor_scalar_max(res1[:], acc1[:], 0.0)
-                nc.sync.dma_start(out[0:P, halves[1]], res1[:])
-            else:
-                nc.scalar.activation(res1[:], acc1[:], ACT.Relu)
-                nc.scalar.dma_start(out[P:N, halves[1]], res1[:])
+            second_product(out_first[:, b, :], 0, b)
+        nc.scalar.activation(res_first[:], out_first[:], ACT.Relu)
+        nc.sync.dma_start(out[:, halves[0]].rearrange("(b p) v -> p b v", p=P), res_first[:])
+
+        out_upper = psum.tile([P, HALF_V], F32, name="out_upper")
+        res_upper = sb.tile([P, HALF_V], F32, name="res_upper")
+        second_product(out_upper[:], 1, 0)
+        nc.vector.tensor_scalar_max(res_upper[:], out_upper[:], 0.0)
+        nc.sync.dma_start(out[0:P, halves[1]], res_upper[:])
+        out_lower = psum.tile([P, HALF_V], F32, name="out_lower")
+        res_lower = sb.tile([P, HALF_V], F32, name="res_lower")
+        second_product(out_lower[:], 1, 1)
+        nc.scalar.activation(res_lower[:], out_lower[:], ACT.Relu)
+        nc.scalar.dma_start(out[P:N, halves[1]], res_lower[:])

@@ -28,6 +28,12 @@ GPSIMD_CLEARS = 128
 SCALAR_DEALS = 72
 
 
+HALF_H = H // 2
+HALF_P = P // 2
+SCALAR_LATE = 22
+W2_EARLY = 192
+
+
 def tile_picked_ytrim_relu_p_kernel(
     tc, x_words, x_scales, w1, w2, offs, pos1, pos2, pos3, out
 ):
@@ -43,20 +49,18 @@ def tile_picked_ytrim_relu_p_kernel(
         scale_win = sb.tile([P, T], U8, name="scale_win", align_bytes=ALIGN)
         word_win = sb.tile([P, T], I32, name="word_win", align_bytes=ALIGN)
         w1_raw = sb.tile([P, PACK, H], F32, name="w1_raw")
+        w2_raw = sb.tile([P, PACK, N], F32, name="w2_raw", tag="w2_then_g2", align_bytes=ALIGN)
 
         nc.gpsimd.memset(scale_win[:].bitcast(I32)[:, 0:GPSIMD_CLEARS], 0)
         nc.vector.memset(scale_win[:].bitcast(I32)[:, GPSIMD_CLEARS : T // 4], 0)
 
         nc.sync.dma_start(offs_sb[:], offs)
         nc.sync.dma_start(w1_raw[:], w1.rearrange("(p j) c -> p j c", j=PACK))
-        for q in range(P // QUADRANT):
-            nc.sync.dma_start(
-                scale_win[QUADRANT * q : QUADRANT * q + 4, :].bitcast(I32),
-                x_scales[0, 4 * q : 4 * q + 4, :].bitcast(I32),
-            )
+        scale_rows = x_scales[0].rearrange("(q r) c -> r q c", r=4)
+        for r in range(4):
+            nc.sync.dma_start(scale_win[r:P:QUADRANT, :].bitcast(I32), scale_rows[r].bitcast(I32))
         nc.sync.dma_start(pos_sb[0][:], pos1)
         nc.sync.dma_start(word_win[:], x_words[0].rearrange("p n t -> p (n t)").bitcast(I32))
-        w2_raw = sb.tile([P, PACK, N], F32, name="w2_raw")
         nc.sync.dma_start(w2_raw[:], w2.rearrange("(p j) n -> p j n", j=PACK))
         nc.sync.dma_start(pos_sb[1][:], pos2)
         nc.sync.dma_start(pos_sb[2][:], pos3)
@@ -69,7 +73,7 @@ def tile_picked_ytrim_relu_p_kernel(
         w1_src = w1_raw[:].rearrange("p j (m t) -> p m j t", t=PACK)
         nc.scalar.copy(w1_dst[:, 0:SCALAR_DEALS], w1_src[:, 0:SCALAR_DEALS])
         nc.vector.tensor_copy(w1_dst[:, SCALAR_DEALS:P], w1_src[:, SCALAR_DEALS:P])
-        w1_q = sb.tile([P, H], U32, name="w1_q", align_bytes=ALIGN)
+        w1_q = sb.tile([P, H], U32, name="w1_q", tag="w1_then_w2", align_bytes=ALIGN)
         w1_sc = sb.tile([P, H], U8, name="w1_sc", align_bytes=ALIGN)
         nc.vector.quantize_mx(out=w1_q[:].bitcast(FP8X4), scales=w1_sc[:], in_=w1_bf[:])
 
@@ -81,14 +85,17 @@ def tile_picked_ytrim_relu_p_kernel(
                 word_win[:].bitcast(U32).indirect(offs_sb[:, a * list_cols : (a + 1) * list_cols]),
             )
 
-        w2_bf = sb.tile([P, N * PACK], BF16, name="w2_bf", align_bytes=ALIGN)
-        nc.vector.tensor_copy(
-            w2_bf[:].rearrange("p (c r j) -> p c j r", r=RUN, j=PACK),
-            w2_raw[:].rearrange("p j (c r) -> p c j r", r=RUN),
-        )
         w2_q = sb.tile([P, N], U32, name="w2_q", align_bytes=ALIGN)
         w2_sc = sb.tile([P, N], U8, name="w2_sc", align_bytes=ALIGN)
-        nc.vector.quantize_mx(out=w2_q[:].bitcast(FP8X4), scales=w2_sc[:], in_=w2_bf[:])
+        w2_src = w2_raw[:].rearrange("p j (c r) -> p c j r", r=RUN)
+        w2_bf = sb.tile([P, W2_EARLY * PACK], BF16, name="w2_bf", align_bytes=ALIGN)
+        nc.vector.tensor_copy(
+            w2_bf[:].rearrange("p (c r j) -> p c j r", r=RUN, j=PACK), w2_src[:, 0 : W2_EARLY // RUN]
+        )
+        for c0, c1 in ((0, P), (P, W2_EARLY)):
+            nc.vector.quantize_mx(
+                out=w2_q[:, c0:c1].bitcast(FP8X4), scales=w2_sc[:, c0:c1], in_=w2_bf[:, c0 * PACK : c1 * PACK]
+            )
 
         def first_product(acc, t, a, c0, c1):
             group = slice(t * P, (t + 1) * P)
@@ -114,40 +121,57 @@ def tile_picked_ytrim_relu_p_kernel(
                 first_product(h_bank[:, a, :], t, a, 0, HALF_S)
             nc.scalar.copy(h[t][:], h_bank[:].rearrange("p a c -> p (a c)"))
 
-        g = [sb.tile([P, PACK, V], BF16, name="g%d" % d, align_bytes=ALIGN) for d in range(3)]
-        hi = sb.tile([P, PACK, V], BF16, name="hi", align_bytes=ALIGN)
-        lo = sb.tile([P, PACK, V], BF16, name="lo", align_bytes=ALIGN)
-        capped = sb.tile([P, PACK, V], BF16, name="capped", align_bytes=ALIGN)
-        halves = [slice(u * HALF_V, (u + 1) * HALF_V) for u in range(2)]
-        for t in range(PACK):
-            for d in range(3):
-                nc.vector.tensor_copy(g[d][:, t, :], h[t][:].indirect(pos_sb[d][:]))
+        w2_late = sb.tile([P, (N - W2_EARLY) * PACK], BF16, name="w2_late", tag="w1_then_w2", align_bytes=ALIGN)
+        nc.scalar.copy(
+            w2_late[:].rearrange("p (c r j) -> p c j r", r=RUN, j=PACK), w2_src[:, W2_EARLY // RUN : N // RUN]
+        )
 
+        g = [sb.tile([P, PACK, V], BF16, name="g%d" % d, align_bytes=ALIGN) for d in range(2)]
+        g.append(sb.tile([P, PACK, V], BF16, name="g2", tag="w2_then_g2", align_bytes=ALIGN))
+        woven = [sb.tile([P, V * PACK], BF16, name="woven%d" % d, align_bytes=ALIGN) for d in range(2)]
+        woven_last = [sb.tile([P, HALF_V * PACK], BF16, name="woven_last%d" % u, align_bytes=ALIGN) for u in range(2)]
+        hi = sb.tile([P, V * PACK], BF16, name="hi", align_bytes=ALIGN)
+        lo = sb.tile([P, V * PACK], BF16, name="lo", align_bytes=ALIGN)
+
+        def weave(dst, src):
+            nc.scalar.copy(
+                dst.rearrange("p (c r t) -> p c t r", r=RUN, t=PACK), src.rearrange("p t (c r) -> p c t r", r=RUN)
+            )
+
+        for t in range(PACK):
+            for d in range(2):
+                nc.vector.tensor_copy(g[d][:, t, :], h[t][:].indirect(pos_sb[d][:]))
+        for d in range(2):
+            weave(woven[d][:], g[d][:])
+        nc.vector.quantize_mx(out=w2_q[:, W2_EARLY:N].bitcast(FP8X4), scales=w2_sc[:, W2_EARLY:N], in_=w2_late[:])
+        for t in range(PACK):
+            nc.vector.tensor_copy(g[2][:, t, :], h[t][:].indirect(pos_sb[2][:]))
+        for u in range(2):
+            weave(woven_last[u][:], g[2][:, :, u * HALF_V : (u + 1) * HALF_V])
+
+        capped = [sb.tile([P, HALF_V * PACK], BF16, name="capped%d" % u, align_bytes=ALIGN) for u in range(2)]
         z_bf = [sb.tile([P, HALF_V * PACK], BF16, name="z_bf%d" % u, align_bytes=ALIGN) for u in range(2)]
         z_q = [sb.tile([P, HALF_V], U32, name="z_q%d" % u, align_bytes=ALIGN) for u in range(2)]
         z_sc = [sb.tile([P, HALF_V], U8, name="z_sc%d" % u, align_bytes=ALIGN) for u in range(2)]
+        halves = [slice(u * HALF_V, (u + 1) * HALF_V) for u in range(2)]
+        wide = [slice(u * HALF_V * PACK, (u + 1) * HALF_V * PACK) for u in range(2)]
 
         def lower(u):
-            nc.vector.tensor_tensor(lo[:, :, halves[u]], g[0][:, :, halves[u]], g[1][:, :, halves[u]], ALU.min)
+            nc.vector.tensor_tensor(lo[:, wide[u]], woven[0][:, wide[u]], woven[1][:, wide[u]], ALU.min)
 
         def cap(u):
-            nc.vector.tensor_tensor(capped[:, :, halves[u]], hi[:, :, halves[u]], g[2][:, :, halves[u]], ALU.min)
+            nc.vector.tensor_tensor(capped[u][:], hi[:, wide[u]], woven_last[u][:], ALU.min)
 
         def median(u, v0, v1):
-            cols = slice(u * HALF_V + v0, u * HALF_V + v1)
-            nc.vector.tensor_tensor(
-                z_bf[u][:, v0 * PACK : v1 * PACK].rearrange("p (c r t) -> p c t r", r=RUN, t=PACK),
-                capped[:, :, cols].rearrange("p t (c r) -> p c t r", r=RUN),
-                lo[:, :, cols].rearrange("p t (c r) -> p c t r", r=RUN),
-                ALU.max,
-            )
+            cols = slice(v0 * PACK, v1 * PACK)
+            nc.vector.tensor_tensor(z_bf[u][:, cols], capped[u][:, cols], lo[:, wide[u]][:, cols], ALU.max)
 
         def quantise(u, v0, v1):
             nc.vector.quantize_mx(
                 out=z_q[u][:, v0:v1].bitcast(FP8X4), scales=z_sc[u][:, v0:v1], in_=z_bf[u][:, v0 * PACK : v1 * PACK]
             )
 
-        nc.vector.tensor_tensor(hi[:], g[0][:], g[1][:], ALU.max)
+        nc.vector.tensor_tensor(hi[:], woven[0][:], woven[1][:], ALU.max)
         lower(0)
         cap(0)
         lower(1)

@@ -48,34 +48,47 @@ def tile_picked_ytrim_relu_p_kernel(
 
         scale_win = sb.tile([P, T], U8, name="scale_win", align_bytes=ALIGN)
         word_win = sb.tile([P, T], I32, name="word_win", align_bytes=ALIGN)
-        w1_raw = sb.tile([P, PACK, H], F32, name="w1_raw")
+        w1_raw = [
+            sb.tile([P, PACK, HALF_H], F32, name="w1_raw%d" % a, tag="w1_raw%d" % a, align_bytes=ALIGN) for a in range(2)
+        ]
         w2_raw = sb.tile([P, PACK, N], F32, name="w2_raw", tag="w2_then_g2", align_bytes=ALIGN)
 
         nc.gpsimd.memset(scale_win[:].bitcast(I32)[:, 0:GPSIMD_CLEARS], 0)
         nc.vector.memset(scale_win[:].bitcast(I32)[:, GPSIMD_CLEARS : T // 4], 0)
 
         nc.sync.dma_start(offs_sb[:], offs)
-        nc.sync.dma_start(w1_raw[:], w1.rearrange("(p j) c -> p j c", j=PACK))
+        w1_rows = w1.rearrange("(p j) c -> p j c", j=PACK)
+        nc.sync.dma_start(w1_raw[0][:], w1_rows[:, :, 0:HALF_H])
         scale_rows = x_scales[0].rearrange("(q r) c -> r q c", r=4)
         for r in range(4):
             nc.sync.dma_start(scale_win[r:P:QUADRANT, :].bitcast(I32), scale_rows[r].bitcast(I32))
         nc.sync.dma_start(pos_sb[0][:], pos1)
         nc.sync.dma_start(word_win[:], x_words[0].rearrange("p n t -> p (n t)").bitcast(I32))
-        nc.sync.dma_start(w2_raw[:], w2.rearrange("(p j) n -> p j n", j=PACK))
+        nc.sync.dma_start(w1_raw[1][:], w1_rows[:, :, HALF_H:H])
         nc.sync.dma_start(pos_sb[1][:], pos2)
         nc.sync.dma_start(pos_sb[2][:], pos3)
+        nc.sync.dma_start(w2_raw[:], w2.rearrange("(p j) n -> p j n", j=PACK))
 
         x_sc = sb.tile([P, S], U8, name="x_sc", align_bytes=ALIGN)
         nc.vector.tensor_copy(x_sc[:], scale_win[:].indirect(offs_sb[:]))
 
-        w1_bf = sb.tile([P, H * PACK], BF16, name="w1_bf", align_bytes=ALIGN)
-        w1_dst = w1_bf[:].rearrange("p (t m j) -> p m j t", t=PACK, j=PACK)
-        w1_src = w1_raw[:].rearrange("p j (m t) -> p m j t", t=PACK)
-        nc.scalar.copy(w1_dst[:, 0:SCALAR_DEALS], w1_src[:, 0:SCALAR_DEALS])
-        nc.vector.tensor_copy(w1_dst[:, SCALAR_DEALS:P], w1_src[:, SCALAR_DEALS:P])
+        w1_bf = [
+            sb.tile([P, H * PACK // 2], BF16, name="w1_bf%d" % a, tag="w1_bf%d" % a, align_bytes=ALIGN) for a in range(2)
+        ]
         w1_q = sb.tile([P, H], U32, name="w1_q", tag="w1_then_w2", align_bytes=ALIGN)
         w1_sc = sb.tile([P, H], U8, name="w1_sc", align_bytes=ALIGN)
-        nc.vector.quantize_mx(out=w1_q[:].bitcast(FP8X4), scales=w1_sc[:], in_=w1_bf[:])
+        w1_dst = [w1_bf[a][:].rearrange("p (t m j) -> p m j t", t=PACK, j=PACK) for a in range(2)]
+        w1_src = [w1_raw[a][:].rearrange("p j (m t) -> p m j t", t=PACK) for a in range(2)]
+
+        def quantise_w1(a):
+            for c0, c1, first in ((0, P, a * P), (P, P + HALF_P, 2 * P + a * HALF_P), (P + HALF_P, 2 * P, 3 * P + a * HALF_P)):
+                cols = slice(first, first + c1 - c0)
+                nc.vector.quantize_mx(
+                    out=w1_q[:, cols].bitcast(FP8X4), scales=w1_sc[:, cols], in_=w1_bf[a][:, c0 * PACK : c1 * PACK]
+                )
+
+        nc.scalar.copy(w1_dst[0], w1_src[0])
+        quantise_w1(0)
 
         x_q = [sb.tile([P, HALF_S], U32, name="x_q%d" % a, align_bytes=ALIGN) for a in range(2)]
         list_cols = HALF_S // LIST_ROWS
@@ -85,17 +98,9 @@ def tile_picked_ytrim_relu_p_kernel(
                 word_win[:].bitcast(U32).indirect(offs_sb[:, a * list_cols : (a + 1) * list_cols]),
             )
 
-        w2_q = sb.tile([P, N], U32, name="w2_q", align_bytes=ALIGN)
-        w2_sc = sb.tile([P, N], U8, name="w2_sc", align_bytes=ALIGN)
-        w2_src = w2_raw[:].rearrange("p j (c r) -> p c j r", r=RUN)
-        w2_bf = sb.tile([P, W2_EARLY * PACK], BF16, name="w2_bf", align_bytes=ALIGN)
-        nc.vector.tensor_copy(
-            w2_bf[:].rearrange("p (c r j) -> p c j r", r=RUN, j=PACK), w2_src[:, 0 : W2_EARLY // RUN]
-        )
-        for c0, c1 in ((0, P), (P, W2_EARLY)):
-            nc.vector.quantize_mx(
-                out=w2_q[:, c0:c1].bitcast(FP8X4), scales=w2_sc[:, c0:c1], in_=w2_bf[:, c0 * PACK : c1 * PACK]
-            )
+        for t in (0, 2):
+            nc.vector.tensor_copy(w1_dst[1][:, :, :, t : t + 2], w1_src[1][:, :, :, t : t + 2])
+        quantise_w1(1)
 
         def first_product(acc, t, a, c0, c1):
             group = slice(t * P, (t + 1) * P)
@@ -121,13 +126,21 @@ def tile_picked_ytrim_relu_p_kernel(
                 first_product(h_bank[:, a, :], t, a, 0, HALF_S)
             nc.scalar.copy(h[t][:], h_bank[:].rearrange("p a c -> p (a c)"))
 
-        w2_late = sb.tile([P, (N - W2_EARLY) * PACK], BF16, name="w2_late", tag="w1_then_w2", align_bytes=ALIGN)
+        w2_bf = sb.tile([P, N * PACK], BF16, name="w2_bf", tag="w1_then_w2", align_bytes=ALIGN)
         nc.scalar.copy(
-            w2_late[:].rearrange("p (c r j) -> p c j r", r=RUN, j=PACK), w2_src[:, W2_EARLY // RUN : N // RUN]
+            w2_bf[:].rearrange("p (c r j) -> p c j r", r=RUN, j=PACK),
+            w2_raw[:].rearrange("p j (c r) -> p c j r", r=RUN),
         )
+        w2_q = sb.tile([P, N], U32, name="w2_q", align_bytes=ALIGN)
+        w2_sc = sb.tile([P, N], U8, name="w2_sc", align_bytes=ALIGN)
 
-        g = [sb.tile([P, PACK, V], BF16, name="g%d" % d, align_bytes=ALIGN) for d in range(2)]
-        g.append(sb.tile([P, PACK, V], BF16, name="g2", tag="w2_then_g2", align_bytes=ALIGN))
+        g_first = sb.tile([P, 1, PACK, V], BF16, name="g_first", align_bytes=ALIGN)
+        g_rest = sb.tile([P, 2, PACK, V], BF16, name="g_rest", tag="w2_then_g2", align_bytes=ALIGN)
+        g = [g_first[:, 0], g_rest[:, 0], g_rest[:, 1]]
+        astray = [
+            sb.tile([P, 3, V], BF16, name="astray0", tag="w1_raw1", align_bytes=ALIGN),
+            sb.tile([P, 3, V], BF16, name="astray1", align_bytes=ALIGN),
+        ]
         woven = [sb.tile([P, V * PACK], BF16, name="woven%d" % d, align_bytes=ALIGN) for d in range(2)]
         woven_last = [sb.tile([P, HALF_V * PACK], BF16, name="woven_last%d" % u, align_bytes=ALIGN) for u in range(2)]
         hi = sb.tile([P, V * PACK], BF16, name="hi", align_bytes=ALIGN)
@@ -138,14 +151,20 @@ def tile_picked_ytrim_relu_p_kernel(
                 dst.rearrange("p (c r t) -> p c t r", r=RUN, t=PACK), src.rearrange("p t (c r) -> p c t r", r=RUN)
             )
 
-        for t in range(PACK):
-            for d in range(2):
+        for a in range(2):
+            home = slice(a * HALF_P, (a + 1) * HALF_P)
+            for d in range(3):
+                nc.vector.tensor_copy(astray[a][:, d, :], h[a][:].indirect(pos_sb[d][:]))
+            for d0, d1 in ((0, 1), (1, 3)) if a == 0 else ((0, 1), (1, 2), (2, 3)):
+                dst = g_first[home] if d0 == 0 else g_rest[home, d0 - 1 : d1 - 1]
+                for t in range(2):
+                    nc.sync.dma_start(dst[:, :, t, :], astray[a][t * HALF_P : (t + 1) * HALF_P, d0:d1, :])
+        for d in range(3):
+            for t in range(2, PACK):
                 nc.vector.tensor_copy(g[d][:, t, :], h[t][:].indirect(pos_sb[d][:]))
-        for d in range(2):
-            weave(woven[d][:], g[d][:])
-        nc.vector.quantize_mx(out=w2_q[:, W2_EARLY:N].bitcast(FP8X4), scales=w2_sc[:, W2_EARLY:N], in_=w2_late[:])
-        for t in range(PACK):
-            nc.vector.tensor_copy(g[2][:, t, :], h[t][:].indirect(pos_sb[2][:]))
+            if d < 2:
+                weave(woven[d][:], g[d])
+        nc.vector.quantize_mx(out=w2_q[:].bitcast(FP8X4), scales=w2_sc[:], in_=w2_bf[:])
         for u in range(2):
             weave(woven_last[u][:], g[2][:, :, u * HALF_V : (u + 1) * HALF_V])
 

@@ -46,7 +46,7 @@ def tile_picked_ytrim_relu_p_kernel(
         offs_sb = lists.tile([P, S // LIST_ROWS], U16, name="offs_sb")
         pos_sb = [lists.tile([P, V // LIST_ROWS], U16, name="pos_sb%d" % d) for d in range(3)]
 
-        scale_win = sb.tile([P, T], U8, name="scale_win", align_bytes=ALIGN)
+        scale_win = sb.tile([P, T], U8, name="scale_win", tag="scales", align_bytes=ALIGN)
         word_win = sb.tile([P, T], I32, name="word_win", align_bytes=ALIGN)
         w1_raw = [
             sb.tile([P, PACK, HALF_H], F32, name="w1_raw%d" % a, tag="w1_raw%d" % a, align_bytes=ALIGN) for a in range(2)
@@ -56,9 +56,9 @@ def tile_picked_ytrim_relu_p_kernel(
         nc.gpsimd.memset(scale_win[:].bitcast(I32)[:, 0:GPSIMD_CLEARS], 0)
         nc.vector.memset(scale_win[:].bitcast(I32)[:, GPSIMD_CLEARS : T // 4], 0)
 
-        nc.sync.dma_start(offs_sb[:], offs)
         w1_rows = w1.rearrange("(p j) c -> p j c", j=PACK)
         nc.sync.dma_start(w1_raw[0][:], w1_rows[:, :, 0:HALF_H])
+        nc.sync.dma_start(offs_sb[:], offs)
         scale_rows = x_scales[0].rearrange("(q r) c -> r q c", r=4)
         for r in range(4):
             nc.sync.dma_start(scale_win[r:P:QUADRANT, :].bitcast(I32), scale_rows[r].bitcast(I32))
@@ -76,7 +76,7 @@ def tile_picked_ytrim_relu_p_kernel(
             sb.tile([P, H * PACK // 2], BF16, name="w1_bf%d" % a, tag="w1_bf%d" % a, align_bytes=ALIGN) for a in range(2)
         ]
         w1_q = sb.tile([P, H], U32, name="w1_q", tag="w1_then_w2", align_bytes=ALIGN)
-        w1_sc = sb.tile([P, H], U8, name="w1_sc", align_bytes=ALIGN)
+        w1_sc = sb.tile([P, H], U8, name="w1_sc", tag="scales", align_bytes=ALIGN)
         w1_dst = [w1_bf[a][:].rearrange("p (t m j) -> p m j t", t=PACK, j=PACK) for a in range(2)]
         w1_src = [w1_raw[a][:].rearrange("p j (m t) -> p m j t", t=PACK) for a in range(2)]
 
@@ -175,32 +175,14 @@ def tile_picked_ytrim_relu_p_kernel(
         halves = [slice(u * HALF_V, (u + 1) * HALF_V) for u in range(2)]
         wide = [slice(u * HALF_V * PACK, (u + 1) * HALF_V * PACK) for u in range(2)]
 
-        def lower(u):
-            nc.vector.tensor_tensor(lo[:, wide[u]], woven[0][:, wide[u]], woven[1][:, wide[u]], ALU.min)
-
-        def cap(u):
-            nc.vector.tensor_tensor(capped[u][:], hi[:, wide[u]], woven_last[u][:], ALU.min)
-
-        def median(u, v0, v1):
-            cols = slice(v0 * PACK, v1 * PACK)
-            nc.vector.tensor_tensor(z_bf[u][:, cols], capped[u][:, cols], lo[:, wide[u]][:, cols], ALU.max)
-
-        def quantise(u, v0, v1):
-            nc.vector.quantize_mx(
-                out=z_q[u][:, v0:v1].bitcast(FP8X4), scales=z_sc[u][:, v0:v1], in_=z_bf[u][:, v0 * PACK : v1 * PACK]
-            )
-
         nc.vector.tensor_tensor(hi[:], woven[0][:], woven[1][:], ALU.max)
-        lower(0)
-        cap(0)
-        lower(1)
-        median(0, 0, HALF_V)
-        cap(1)
-        quantise(0, 0, HALF_V)
-        median(1, 0, QUARTER_V)
-        median(1, QUARTER_V, HALF_V)
-        quantise(1, 0, QUARTER_V)
-        quantise(1, QUARTER_V, HALF_V)
+        nc.vector.tensor_tensor(lo[:], woven[0][:], woven[1][:], ALU.min)
+        for u in range(2):
+            nc.vector.tensor_tensor(capped[u][:], hi[:, wide[u]], woven_last[u][:], ALU.min)
+        for u in range(2):
+            nc.vector.tensor_tensor(z_bf[u][:], capped[u][:], lo[:, wide[u]], ALU.max)
+        for u in range(2):
+            nc.vector.quantize_mx(out=z_q[u][:].bitcast(FP8X4), scales=z_sc[u][:], in_=z_bf[u][:])
 
         def second_product(acc, u, b):
             features = slice(b * P, (b + 1) * P)
@@ -209,20 +191,16 @@ def tile_picked_ytrim_relu_p_kernel(
                 rhs=z_q[u][:].bitcast(FP8X4), rhs_scale=z_sc[u][:], start=True, stop=True,
             )
 
+        res = sb.tile([P, 2, V], F32, name="res")
         out_first = psum.tile([P, 2, HALF_V], F32, name="out_first", tag="reused_bank")
-        res_first = sb.tile([P, 2, HALF_V], F32, name="res_first")
         for b in range(2):
             second_product(out_first[:, b, :], 0, b)
-        nc.scalar.activation(res_first[:], out_first[:], ACT.Relu)
-        nc.sync.dma_start(out[:, halves[0]].rearrange("(b p) v -> p b v", p=P), res_first[:])
-
+        nc.scalar.activation(res[:, :, halves[0]], out_first[:], ACT.Relu)
         out_upper = psum.tile([P, HALF_V], F32, name="out_upper")
-        res_upper = sb.tile([P, HALF_V], F32, name="res_upper")
         second_product(out_upper[:], 1, 0)
-        nc.vector.tensor_scalar_max(res_upper[:], out_upper[:], 0.0)
-        nc.sync.dma_start(out[0:P, halves[1]], res_upper[:])
+        nc.vector.tensor_scalar_max(res[:, 0, halves[1]], out_upper[:], 0.0)
+        nc.sync.dma_start(out[0:P, :], res[:, 0, :])
         out_lower = psum.tile([P, HALF_V], F32, name="out_lower")
-        res_lower = sb.tile([P, HALF_V], F32, name="res_lower")
         second_product(out_lower[:], 1, 1)
-        nc.scalar.activation(res_lower[:], out_lower[:], ACT.Relu)
-        nc.scalar.dma_start(out[P:N, halves[1]], res_lower[:])
+        nc.scalar.activation(res[:, 1, halves[1]], out_lower[:], ACT.Relu)
+        nc.scalar.dma_start(out[P:N, :], res[:, 1, :])

@@ -128,8 +128,8 @@ def tile_picked_ytrim_relu_p_kernel(
 
         w2_bf = sb.tile([P, N * PACK], BF16, name="w2_bf", tag="w1_then_w2", align_bytes=ALIGN)
         nc.scalar.copy(
-            w2_bf[:].rearrange("p (c r j) -> p c j r", r=RUN, j=PACK),
-            w2_raw[:].rearrange("p j (c r) -> p c j r", r=RUN),
+            w2_bf[:].rearrange("p (b m j) -> p m j b", b=2, j=PACK),
+            w2_raw[:].rearrange("p j (m b) -> p m j b", b=2),
         )
         w2_q = sb.tile([P, N], U32, name="w2_q", align_bytes=ALIGN)
         w2_sc = sb.tile([P, N], U8, name="w2_sc", align_bytes=ALIGN)
@@ -199,8 +199,7 @@ def tile_picked_ytrim_relu_p_kernel(
         out_upper = psum.tile([P, HALF_V], F32, name="out_upper")
         second_product(out_upper[:], 1, 0)
         nc.vector.tensor_scalar_max(res[:, 0, halves[1]], out_upper[:], 0.0)
-        nc.sync.dma_start(out[0:P, :], res[:, 0, :])
         out_lower = psum.tile([P, HALF_V], F32, name="out_lower")
         second_product(out_lower[:], 1, 1)
         nc.scalar.activation(res[:, 1, halves[1]], out_lower[:], ACT.Relu)
-        nc.scalar.dma_start(out[P:N, :], res[:, 1, :])
+        nc.sync.dma_start(out.rearrange("(p b) v -> p b v", b=2), res[:])

@@ -51,7 +51,9 @@ def tile_picked_ytrim_relu_p_kernel(
         w1_raw = [
             sb.tile([P, PACK, HALF_H], F32, name="w1_raw%d" % a, tag="w1_raw%d" % a, align_bytes=ALIGN) for a in range(2)
         ]
-        w2_raw = sb.tile([P, PACK, N], F32, name="w2_raw", tag="w2_then_g2", align_bytes=ALIGN)
+        w2_raw = [
+            sb.tile([P, PACK, P], F32, name="w2_raw%d" % e, tag=("w2_then_g2", "w2_raw1")[e], align_bytes=ALIGN) for e in range(2)
+        ]
 
         nc.gpsimd.memset(scale_win[:].bitcast(I32)[:, 0:GPSIMD_CLEARS], 0)
         nc.vector.memset(scale_win[:].bitcast(I32)[:, GPSIMD_CLEARS : T // 4], 0)
@@ -67,7 +69,8 @@ def tile_picked_ytrim_relu_p_kernel(
         nc.sync.dma_start(w1_raw[1][:], w1_rows[:, :, HALF_H:H])
         nc.sync.dma_start(pos_sb[1][:], pos2)
         nc.sync.dma_start(pos_sb[2][:], pos3)
-        nc.sync.dma_start(w2_raw[:], w2.rearrange("(p j) n -> p j n", j=PACK))
+        for e in range(2):
+            nc.sync.dma_start(w2_raw[e][:], w2.rearrange("(p j) n -> p j n", j=PACK)[:, :, e * P : (e + 1) * P])
 
         x_sc = sb.tile([P, S], U8, name="x_sc", align_bytes=ALIGN)
         nc.vector.tensor_copy(x_sc[:], scale_win[:].indirect(offs_sb[:]))
@@ -127,10 +130,11 @@ def tile_picked_ytrim_relu_p_kernel(
             nc.scalar.copy(h[t][:], h_bank[:].rearrange("p a c -> p (a c)"))
 
         w2_bf = sb.tile([P, N * PACK], BF16, name="w2_bf", tag="w1_then_w2", align_bytes=ALIGN)
-        nc.scalar.copy(
-            w2_bf[:].rearrange("p (b m j) -> p m j b", b=2, j=PACK),
-            w2_raw[:].rearrange("p j (m b) -> p m j b", b=2),
-        )
+        for e in range(2):
+            nc.scalar.copy(
+                w2_bf[:].rearrange("p (b m j) -> p m j b", b=2, j=PACK)[:, e * HALF_P : (e + 1) * HALF_P],
+                w2_raw[e][:].rearrange("p j (m b) -> p m j b", b=2),
+            )
         w2_q = sb.tile([P, N], U32, name="w2_q", align_bytes=ALIGN)
         w2_sc = sb.tile([P, N], U8, name="w2_sc", align_bytes=ALIGN)
 

@@ -19,19 +19,12 @@ P = 128
 PACK = 4
 LIST_ROWS = 16
 QUADRANT = 32
-HALF_S = S // 2
+PIECE = 128
+PIECES = S // PIECE
 HALF_V = V // 2
-QUARTER_V = V // 4
 RUN = 4
 ALIGN = 64
 GPSIMD_CLEARS = 128
-SCALAR_DEALS = 72
-
-
-HALF_H = H // 2
-HALF_P = P // 2
-SCALAR_LATE = 22
-W2_EARLY = 192
 
 
 def tile_picked_ytrim_relu_p_kernel(
@@ -46,146 +39,118 @@ def tile_picked_ytrim_relu_p_kernel(
         offs_sb = lists.tile([P, S // LIST_ROWS], U16, name="offs_sb")
         pos_sb = [lists.tile([P, V // LIST_ROWS], U16, name="pos_sb%d" % d) for d in range(3)]
 
-        scale_win = sb.tile([P, T], U8, name="scale_win", tag="scales", align_bytes=ALIGN)
+        scale_win = sb.tile([P, T], U8, name="scale_win", align_bytes=ALIGN)
         word_win = sb.tile([P, T], I32, name="word_win", align_bytes=ALIGN)
-        w1_raw = [
-            sb.tile([P, PACK, HALF_H], F32, name="w1_raw%d" % a, tag="w1_raw%d" % a, align_bytes=ALIGN) for a in range(2)
-        ]
-        w2_raw = [
-            sb.tile([P, PACK, P], F32, name="w2_raw%d" % e, tag=("w2_then_g2", "w2_raw1")[e], align_bytes=ALIGN) for e in range(2)
-        ]
+        w1_raw = [sb.tile([P, 2, H], F32, name="w1_raw%d" % a, align_bytes=ALIGN) for a in range(2)]
+        w2_raw = sb.tile([P, PACK, N], F32, name="w2_raw", align_bytes=ALIGN)
 
         nc.gpsimd.memset(scale_win[:].bitcast(I32)[:, 0:GPSIMD_CLEARS], 0)
         nc.vector.memset(scale_win[:].bitcast(I32)[:, GPSIMD_CLEARS : T // 4], 0)
 
         w1_rows = w1.rearrange("(p j) c -> p j c", j=PACK)
-        nc.sync.dma_start(w1_raw[0][:], w1_rows[:, :, 0:HALF_H])
+        nc.sync.dma_start(w1_raw[0][:], w1_rows[:, 0:2, :])
         nc.sync.dma_start(offs_sb[:], offs)
         scale_rows = x_scales[0].rearrange("(q r) c -> r q c", r=4)
         for r in range(4):
             nc.sync.dma_start(scale_win[r:P:QUADRANT, :].bitcast(I32), scale_rows[r].bitcast(I32))
-        nc.sync.dma_start(pos_sb[0][:], pos1)
+        nc.sync.dma_start(w1_raw[1][:], w1_rows[:, 2:4, :])
         nc.sync.dma_start(word_win[:], x_words[0].rearrange("p n t -> p (n t)").bitcast(I32))
-        nc.sync.dma_start(w1_raw[1][:], w1_rows[:, :, HALF_H:H])
-        nc.sync.dma_start(pos_sb[1][:], pos2)
-        nc.sync.dma_start(pos_sb[2][:], pos3)
-        for e in range(2):
-            nc.sync.dma_start(w2_raw[e][:], w2.rearrange("(p j) n -> p j n", j=PACK)[:, :, e * P : (e + 1) * P])
+        for d, pos in enumerate((pos1, pos2, pos3)):
+            nc.sync.dma_start(pos_sb[d][:], pos)
+        nc.sync.dma_start(w2_raw[:], w2.rearrange("(p j) n -> p j n", j=PACK))
 
         x_sc = sb.tile([P, S], U8, name="x_sc", align_bytes=ALIGN)
         nc.vector.tensor_copy(x_sc[:], scale_win[:].indirect(offs_sb[:]))
 
-        w1_bf = [
-            sb.tile([P, H * PACK // 2], BF16, name="w1_bf%d" % a, tag="w1_bf%d" % a, align_bytes=ALIGN) for a in range(2)
-        ]
-        w1_q = sb.tile([P, H], U32, name="w1_q", tag="w1_then_w2", align_bytes=ALIGN)
-        w1_sc = sb.tile([P, H], U8, name="w1_sc", tag="scales", align_bytes=ALIGN)
-        w1_dst = [w1_bf[a][:].rearrange("p (t m j) -> p m j t", t=PACK, j=PACK) for a in range(2)]
+        w1_bf = sb.tile([P, H * PACK], BF16, name="w1_bf", align_bytes=ALIGN)
+        w1_q = sb.tile([P, H], U32, name="w1_q", align_bytes=ALIGN)
+        w1_sc = sb.tile([P, H], U8, name="w1_sc", align_bytes=ALIGN)
+        w1_dst = w1_bf[:].rearrange("p (t m j) -> p m j t", t=PACK, j=PACK)
         w1_src = [w1_raw[a][:].rearrange("p j (m t) -> p m j t", t=PACK) for a in range(2)]
+        nc.scalar.copy(w1_dst[:, :, 0:2, :], w1_src[0])
+        nc.scalar.copy(w1_dst[:, 0 : P // 2, 2:4, :], w1_src[1][:, 0 : P // 2])
+        nc.vector.tensor_copy(w1_dst[:, P // 2 : P, 2:4, :], w1_src[1][:, P // 2 : P])
+        nc.vector.quantize_mx(out=w1_q[:].bitcast(FP8X4), scales=w1_sc[:], in_=w1_bf[:])
 
-        def quantise_w1(a):
-            for c0, c1, first in ((0, P, a * P), (P, P + HALF_P, 2 * P + a * HALF_P), (P + HALF_P, 2 * P, 3 * P + a * HALF_P)):
-                cols = slice(first, first + c1 - c0)
-                nc.vector.quantize_mx(
-                    out=w1_q[:, cols].bitcast(FP8X4), scales=w1_sc[:, cols], in_=w1_bf[a][:, c0 * PACK : c1 * PACK]
-                )
-
-        nc.scalar.copy(w1_dst[0], w1_src[0])
-        quantise_w1(0)
-
-        x_q = [sb.tile([P, HALF_S], U32, name="x_q%d" % a, align_bytes=ALIGN) for a in range(2)]
-        list_cols = HALF_S // LIST_ROWS
-        for a in range(2):
+        x_q = [sb.tile([P, PIECE], U32, name="x_q%d" % a, align_bytes=ALIGN) for a in range(PIECES)]
+        list_cols = PIECE // LIST_ROWS
+        for a in range(PIECES):
             nc.vector.tensor_copy(
-                x_q[a][:],
-                word_win[:].bitcast(U32).indirect(offs_sb[:, a * list_cols : (a + 1) * list_cols]),
+                x_q[a][:], word_win[:].bitcast(U32).indirect(offs_sb[:, a * list_cols : (a + 1) * list_cols])
             )
 
-        for t in (0, 2):
-            nc.vector.tensor_copy(w1_dst[1][:, :, :, t : t + 2], w1_src[1][:, :, :, t : t + 2])
-        quantise_w1(1)
-
-        def first_product(acc, t, a, c0, c1):
+        def first_product(acc, t, a):
             group = slice(t * P, (t + 1) * P)
             nc.tensor.matmul_mx(
                 out=acc, lhsT=w1_q[:, group].bitcast(FP8X4), lhsT_scale=w1_sc[:, group],
-                rhs=x_q[a][:, c0:c1].bitcast(FP8X4), rhs_scale=x_sc[:, a * HALF_S + c0 : a * HALF_S + c1],
+                rhs=x_q[a][:].bitcast(FP8X4), rhs_scale=x_sc[:, a * PIECE : (a + 1) * PIECE],
                 start=True, stop=True,
             )
 
         h = [sb.tile([P, S], F32, name="h%d" % t) for t in range(PACK)]
-        h0_first = psum.tile([P, HALF_S], F32, name="h0_first", tag="reused_bank")
-        first_product(h0_first[:], 0, 0, 0, HALF_S)
-        nc.scalar.copy(h[0][:, 0:HALF_S], h0_first[:])
-        h0_second = psum.tile([P, P], F32, name="h0_second")
-        first_product(h0_second[:], 0, 1, 0, P)
-        nc.scalar.copy(h[0][:, HALF_S : HALF_S + P], h0_second[:])
-        h0_third = psum.tile([P, P], F32, name="h0_third")
-        first_product(h0_third[:], 0, 1, P, HALF_S)
-        nc.scalar.copy(h[0][:, HALF_S + P :], h0_third[:])
-        for t in range(1, PACK):
-            h_bank = psum.tile([P, 2, HALF_S], F32, name="h_bank%d" % t)
-            for a in range(2):
-                first_product(h_bank[:, a, :], t, a, 0, HALF_S)
-            nc.scalar.copy(h[t][:], h_bank[:].rearrange("p a c -> p (a c)"))
+        for a in range(PIECES - 1):
+            early = psum.tile([P, 2, PIECE], F32, name="early%d" % a, tag="bank%d" % a)
+            for t in range(2):
+                first_product(early[:, t, :], t, a)
+            for t in range(2):
+                nc.scalar.copy(h[t][:, a * PIECE : (a + 1) * PIECE], early[:, t, :])
+        for t in range(2):
+            last = psum.tile([P, PIECE], F32, name="last%d" % t, tag="bank%d" % (3 + t))
+            first_product(last[:], t, PIECES - 1)
+            nc.scalar.copy(h[t][:, S - PIECE : S], last[:])
+        for t in range(2, PACK):
+            late = psum.tile([P, PIECES, PIECE], F32, name="late%d" % t, tag="bank%d" % (3 + t))
+            for a in range(PIECES):
+                first_product(late[:, a, :], t, a)
+            nc.scalar.copy(h[t][:], late[:].rearrange("p a c -> p (a c)"))
 
-        w2_bf = sb.tile([P, N * PACK], BF16, name="w2_bf", tag="w1_then_w2", align_bytes=ALIGN)
-        for e in range(2):
-            nc.scalar.copy(
-                w2_bf[:].rearrange("p (b m j) -> p m j b", b=2, j=PACK)[:, e * HALF_P : (e + 1) * HALF_P],
-                w2_raw[e][:].rearrange("p j (m b) -> p m j b", b=2),
-            )
+        w2_bf = sb.tile([P, N * PACK], BF16, name="w2_bf", align_bytes=ALIGN)
         w2_q = sb.tile([P, N], U32, name="w2_q", align_bytes=ALIGN)
         w2_sc = sb.tile([P, N], U8, name="w2_sc", align_bytes=ALIGN)
+        nc.vector.tensor_copy(
+            w2_bf[:].rearrange("p (b m j) -> p m j b", b=2, j=PACK), w2_raw[:].rearrange("p j (m b) -> p m j b", b=2)
+        )
 
-        g_first = sb.tile([P, 1, PACK, V], BF16, name="g_first", align_bytes=ALIGN)
-        g_rest = sb.tile([P, 2, PACK, V], BF16, name="g_rest", tag="w2_then_g2", align_bytes=ALIGN)
-        g = [g_first[:, 0], g_rest[:, 0], g_rest[:, 1]]
-        astray = [
-            sb.tile([P, 3, V], BF16, name="astray0", tag="w1_raw1", align_bytes=ALIGN),
-            sb.tile([P, 3, V], BF16, name="astray1", align_bytes=ALIGN),
-        ]
-        woven = [sb.tile([P, V * PACK], BF16, name="woven%d" % d, align_bytes=ALIGN) for d in range(2)]
-        woven_last = [sb.tile([P, HALF_V * PACK], BF16, name="woven_last%d" % u, align_bytes=ALIGN) for u in range(2)]
-        hi = sb.tile([P, V * PACK], BF16, name="hi", align_bytes=ALIGN)
-        lo = sb.tile([P, V * PACK], BF16, name="lo", align_bytes=ALIGN)
+        g = [sb.tile([P, PACK, V], BF16, name="g%d" % d, align_bytes=ALIGN) for d in range(3)]
+        hi = sb.tile([P, PACK, V], BF16, name="hi", align_bytes=ALIGN)
+        lo = sb.tile([P, PACK, V], BF16, name="lo", align_bytes=ALIGN)
+        capped = sb.tile([P, PACK, V], BF16, name="capped", align_bytes=ALIGN)
+        halves = [slice(u * HALF_V, (u + 1) * HALF_V) for u in range(2)]
+        half_cols = HALF_V // LIST_ROWS
 
-        def weave(dst, src):
-            nc.scalar.copy(
-                dst.rearrange("p (c r t) -> p c t r", r=RUN, t=PACK), src.rearrange("p t (c r) -> p c t r", r=RUN)
-            )
-
-        for a in range(2):
-            home = slice(a * HALF_P, (a + 1) * HALF_P)
-            for d in range(3):
-                nc.vector.tensor_copy(astray[a][:, d, :], h[a][:].indirect(pos_sb[d][:]))
-            for d0, d1 in ((0, 1), (1, 3)) if a == 0 else ((0, 1), (1, 2), (2, 3)):
-                dst = g_first[home] if d0 == 0 else g_rest[home, d0 - 1 : d1 - 1]
-                for t in range(2):
-                    nc.sync.dma_start(dst[:, :, t, :], astray[a][t * HALF_P : (t + 1) * HALF_P, d0:d1, :])
-        for d in range(3):
-            for t in range(2, PACK):
-                nc.vector.tensor_copy(g[d][:, t, :], h[t][:].indirect(pos_sb[d][:]))
-            if d < 2:
-                weave(woven[d][:], g[d])
-        nc.vector.quantize_mx(out=w2_q[:].bitcast(FP8X4), scales=w2_sc[:], in_=w2_bf[:])
+        for t, d in ((0, 0), (0, 1), (0, 2), (1, 0), (1, 1)):
+            nc.vector.tensor_copy(g[d][:, t, :], h[t][:].indirect(pos_sb[d][:]))
+        for t, d in ((1, 2), (2, 0), (2, 1), (2, 2)):
+            nc.scalar.activation(g[d][:, t, :], h[t][:].indirect(pos_sb[d][:]), ACT.Copy)
         for u in range(2):
-            weave(woven_last[u][:], g[2][:, :, u * HALF_V : (u + 1) * HALF_V])
+            for d in range(3):
+                nc.scalar.activation(
+                    g[d][:, 3, halves[u]], h[3][:].indirect(pos_sb[d][:, u * half_cols : (u + 1) * half_cols]), ACT.Copy
+                )
+        nc.vector.quantize_mx(out=w2_q[:].bitcast(FP8X4), scales=w2_sc[:], in_=w2_bf[:])
 
-        capped = [sb.tile([P, HALF_V * PACK], BF16, name="capped%d" % u, align_bytes=ALIGN) for u in range(2)]
+        def narrow(t0, t1, cols):
+            nc.vector.tensor_tensor(hi[:, t0:t1, cols], g[0][:, t0:t1, cols], g[1][:, t0:t1, cols], ALU.max)
+            nc.vector.tensor_tensor(lo[:, t0:t1, cols], g[0][:, t0:t1, cols], g[1][:, t0:t1, cols], ALU.min)
+            nc.vector.tensor_tensor(capped[:, t0:t1, cols], hi[:, t0:t1, cols], g[2][:, t0:t1, cols], ALU.min)
+
         z_bf = [sb.tile([P, HALF_V * PACK], BF16, name="z_bf%d" % u, align_bytes=ALIGN) for u in range(2)]
         z_q = [sb.tile([P, HALF_V], U32, name="z_q%d" % u, align_bytes=ALIGN) for u in range(2)]
         z_sc = [sb.tile([P, HALF_V], U8, name="z_sc%d" % u, align_bytes=ALIGN) for u in range(2)]
-        halves = [slice(u * HALF_V, (u + 1) * HALF_V) for u in range(2)]
-        wide = [slice(u * HALF_V * PACK, (u + 1) * HALF_V * PACK) for u in range(2)]
 
-        nc.vector.tensor_tensor(hi[:], woven[0][:], woven[1][:], ALU.max)
-        nc.vector.tensor_tensor(lo[:], woven[0][:], woven[1][:], ALU.min)
+        def woven_max(u):
+            nc.vector.tensor_tensor(
+                z_bf[u][:].rearrange("p (c r t) -> p c t r", r=RUN, t=PACK),
+                capped[:, :, halves[u]].rearrange("p t (c r) -> p c t r", r=RUN),
+                lo[:, :, halves[u]].rearrange("p t (c r) -> p c t r", r=RUN),
+                ALU.max,
+            )
+
+        narrow(0, 2, slice(0, V))
+        narrow(2, 3, slice(0, V))
         for u in range(2):
-            nc.vector.tensor_tensor(capped[u][:], hi[:, wide[u]], woven_last[u][:], ALU.min)
-        for u in range(2):
-            nc.vector.tensor_tensor(z_bf[u][:], capped[u][:], lo[:, wide[u]], ALU.max)
-        for u in range(2):
+            narrow(3, 4, halves[u])
+            woven_max(u)
             nc.vector.quantize_mx(out=z_q[u][:].bitcast(FP8X4), scales=z_sc[u][:], in_=z_bf[u][:])
 
         def second_product(acc, u, b):
@@ -196,14 +161,14 @@ def tile_picked_ytrim_relu_p_kernel(
             )
 
         res = sb.tile([P, 2, V], F32, name="res")
-        out_first = psum.tile([P, 2, HALF_V], F32, name="out_first", tag="reused_bank")
+        out_first = psum.tile([P, 2, HALF_V], F32, name="out_first", tag="bank0")
         for b in range(2):
             second_product(out_first[:, b, :], 0, b)
         nc.scalar.activation(res[:, :, halves[0]], out_first[:], ACT.Relu)
-        out_upper = psum.tile([P, HALF_V], F32, name="out_upper")
+        out_upper = psum.tile([P, HALF_V], F32, name="out_upper", tag="bank1")
         second_product(out_upper[:], 1, 0)
         nc.vector.tensor_scalar_max(res[:, 0, halves[1]], out_upper[:], 0.0)
-        out_lower = psum.tile([P, HALF_V], F32, name="out_lower")
+        out_lower = psum.tile([P, HALF_V], F32, name="out_lower", tag="bank2")
         second_product(out_lower[:], 1, 1)
         nc.scalar.activation(res[:, 1, halves[1]], out_lower[:], ACT.Relu)
         nc.sync.dma_start(out.rearrange("(p b) v -> p b v", b=2), res[:])

@@ -22,6 +22,7 @@ QUADRANT = 32
 PIECE = 128
 PIECES = S // PIECE
 HALF_V = V // 2
+CUTS = ((0, 128), (128, 256))
 RUN = 4
 ALIGN = 64
 GPSIMD_CLEARS = 128
@@ -55,15 +56,15 @@ def tile_picked_ytrim_relu_p_kernel(
             nc.sync.dma_start(scale_win[r:P:QUADRANT, :].bitcast(I32), scale_rows[r].bitcast(I32))
         nc.sync.dma_start(w1_raw[1][:], w1_rows[:, 2:4, :])
         nc.sync.dma_start(word_win[:], x_words[0].rearrange("p n t -> p (n t)").bitcast(I32))
+        nc.sync.dma_start(w2_raw[:], w2.rearrange("(p j) n -> p j n", j=PACK))
         for d, pos in enumerate((pos1, pos2, pos3)):
             nc.sync.dma_start(pos_sb[d][:], pos)
-        nc.sync.dma_start(w2_raw[:], w2.rearrange("(p j) n -> p j n", j=PACK))
 
         x_sc = sb.tile([P, S], U8, name="x_sc", align_bytes=ALIGN)
         nc.vector.tensor_copy(x_sc[:], scale_win[:].indirect(offs_sb[:]))
 
         w1_bf = sb.tile([P, H * PACK], BF16, name="w1_bf", align_bytes=ALIGN)
-        w1_q = sb.tile([P, H], U32, name="w1_q", align_bytes=ALIGN)
+        w1_q = sb.tile([P, H], U32, name="w1_q", tag="w1_q", align_bytes=ALIGN)
         w1_sc = sb.tile([P, H], U8, name="w1_sc", align_bytes=ALIGN)
         w1_dst = w1_bf[:].rearrange("p (t m j) -> p m j t", t=PACK, j=PACK)
         w1_src = [w1_raw[a][:].rearrange("p j (m t) -> p m j t", t=PACK) for a in range(2)]
@@ -72,37 +73,38 @@ def tile_picked_ytrim_relu_p_kernel(
         nc.vector.tensor_copy(w1_dst[:, P // 2 : P, 2:4, :], w1_src[1][:, P // 2 : P])
         nc.vector.quantize_mx(out=w1_q[:].bitcast(FP8X4), scales=w1_sc[:], in_=w1_bf[:])
 
-        x_q = [sb.tile([P, PIECE], U32, name="x_q%d" % a, align_bytes=ALIGN) for a in range(PIECES)]
+        x_q = sb.tile([P, S], U32, name="x_q", align_bytes=ALIGN)
         list_cols = PIECE // LIST_ROWS
         for a in range(PIECES):
             nc.vector.tensor_copy(
-                x_q[a][:], word_win[:].bitcast(U32).indirect(offs_sb[:, a * list_cols : (a + 1) * list_cols])
+                x_q[:, a * PIECE : (a + 1) * PIECE],
+                word_win[:].bitcast(U32).indirect(offs_sb[:, a * list_cols : (a + 1) * list_cols]),
             )
 
-        def first_product(acc, t, a):
+        def first_product(acc, t, cols):
             group = slice(t * P, (t + 1) * P)
             nc.tensor.matmul_mx(
                 out=acc, lhsT=w1_q[:, group].bitcast(FP8X4), lhsT_scale=w1_sc[:, group],
-                rhs=x_q[a][:].bitcast(FP8X4), rhs_scale=x_sc[:, a * PIECE : (a + 1) * PIECE],
+                rhs=x_q[:, cols].bitcast(FP8X4), rhs_scale=x_sc[:, cols],
                 start=True, stop=True,
             )
 
         h = [sb.tile([P, S], F32, name="h%d" % t) for t in range(PACK)]
         for a in range(PIECES - 1):
+            cols = slice(a * PIECE, (a + 1) * PIECE)
             early = psum.tile([P, 2, PIECE], F32, name="early%d" % a, tag="bank%d" % a)
             for t in range(2):
-                first_product(early[:, t, :], t, a)
+                first_product(early[:, t, :], t, cols)
             for t in range(2):
-                nc.scalar.copy(h[t][:, a * PIECE : (a + 1) * PIECE], early[:, t, :])
+                nc.scalar.copy(h[t][:, cols], early[:, t, :])
         for t in range(2):
             last = psum.tile([P, PIECE], F32, name="last%d" % t, tag="bank%d" % (3 + t))
-            first_product(last[:], t, PIECES - 1)
+            first_product(last[:], t, slice(S - PIECE, S))
             nc.scalar.copy(h[t][:, S - PIECE : S], last[:])
         for t in range(2, PACK):
-            late = psum.tile([P, PIECES, PIECE], F32, name="late%d" % t, tag="bank%d" % (3 + t))
-            for a in range(PIECES):
-                first_product(late[:, a, :], t, a)
-            nc.scalar.copy(h[t][:], late[:].rearrange("p a c -> p (a c)"))
+            late = psum.tile([P, S], F32, name="late%d" % t, tag="bank%d" % (3 + t))
+            first_product(late[:], t, slice(0, S))
+            nc.scalar.copy(h[t][:], late[:])
 
         w2_bf = sb.tile([P, N * PACK], BF16, name="w2_bf", align_bytes=ALIGN)
         w2_q = sb.tile([P, N], U32, name="w2_q", align_bytes=ALIGN)
@@ -111,47 +113,68 @@ def tile_picked_ytrim_relu_p_kernel(
             w2_bf[:].rearrange("p (b m j) -> p m j b", b=2, j=PACK), w2_raw[:].rearrange("p j (m b) -> p m j b", b=2)
         )
 
-        g = [sb.tile([P, PACK, V], BF16, name="g%d" % d, align_bytes=ALIGN) for d in range(3)]
-        hi = sb.tile([P, PACK, V], BF16, name="hi", align_bytes=ALIGN)
+        g = [sb.tile([P, 2, V], BF16, name="g%d" % d, align_bytes=ALIGN) for d in range(3)]
+        hi = sb.tile([P, 2, V], BF16, name="hi", align_bytes=ALIGN)
         lo = sb.tile([P, PACK, V], BF16, name="lo", align_bytes=ALIGN)
         capped = sb.tile([P, PACK, V], BF16, name="capped", align_bytes=ALIGN)
-        halves = [slice(u * HALF_V, (u + 1) * HALF_V) for u in range(2)]
-        half_cols = HALF_V // LIST_ROWS
+        g_rest = sb.tile([P, 6, 2, HALF_V], BF16, name="g_rest", tag="w1_q", align_bytes=ALIGN)
+        parts = [slice(a, b) for a, b in CUTS]
+        g_late = [[capped[:, 0:2, HALF_V:V], g_rest[:, 0], g_rest[:, 1]], [g_rest[:, 2 + d] for d in range(3)]]
+        g2_late = g_rest[:, 5, 0, :]
+        hi_late = [lo[:, 2:4, HALF_V:V], g_late[0][2]]
 
-        for t, d in ((0, 0), (0, 1), (0, 2), (1, 0), (1, 1)):
+        for t, d in ((0, 0), (0, 1), (1, 0), (1, 1), (0, 2)):
             nc.vector.tensor_copy(g[d][:, t, :], h[t][:].indirect(pos_sb[d][:]))
-        for t, d in ((1, 2), (2, 0), (2, 1), (2, 2)):
-            nc.scalar.activation(g[d][:, t, :], h[t][:].indirect(pos_sb[d][:]), ACT.Copy)
-        for u in range(2):
-            for d in range(3):
-                nc.scalar.activation(
-                    g[d][:, 3, halves[u]], h[3][:].indirect(pos_sb[d][:, u * half_cols : (u + 1) * half_cols]), ACT.Copy
-                )
+        lists_of = [slice(part.start // LIST_ROWS, part.stop // LIST_ROWS) for part in parts]
+        nc.vector.tensor_copy(g[2][:, 1, parts[0]], h[1][:].indirect(pos_sb[2][:, lists_of[0]]))
+        for u, entries in enumerate(lists_of):
+            if u == 1:
+                nc.scalar.activation(g2_late, h[1][:].indirect(pos_sb[2][:, entries]), ACT.Copy)
+            for t, d in ((2, 0), (2, 1), (3, 0), (3, 1), (2, 2), (3, 2)):
+                nc.scalar.activation(g_late[u][d][:, t - 2, :], h[t][:].indirect(pos_sb[d][:, entries]), ACT.Copy)
         nc.vector.quantize_mx(out=w2_q[:].bitcast(FP8X4), scales=w2_sc[:], in_=w2_bf[:])
 
-        def narrow(t0, t1, cols):
-            nc.vector.tensor_tensor(hi[:, t0:t1, cols], g[0][:, t0:t1, cols], g[1][:, t0:t1, cols], ALU.max)
-            nc.vector.tensor_tensor(lo[:, t0:t1, cols], g[0][:, t0:t1, cols], g[1][:, t0:t1, cols], ALU.min)
-            nc.vector.tensor_tensor(capped[:, t0:t1, cols], hi[:, t0:t1, cols], g[2][:, t0:t1, cols], ALU.min)
+        widths = [part.stop - part.start for part in parts]
+        z_bf = [sb.tile([P, w * PACK], BF16, name="z_bf%d" % u, align_bytes=ALIGN) for u, w in enumerate(widths)]
+        z_q = [sb.tile([P, w], U32, name="z_q%d" % u, align_bytes=ALIGN) for u, w in enumerate(widths)]
+        z_sc = [sb.tile([P, w], U8, name="z_sc%d" % u, align_bytes=ALIGN) for u, w in enumerate(widths)]
 
-        z_bf = [sb.tile([P, HALF_V * PACK], BF16, name="z_bf%d" % u, align_bytes=ALIGN) for u in range(2)]
-        z_q = [sb.tile([P, HALF_V], U32, name="z_q%d" % u, align_bytes=ALIGN) for u in range(2)]
-        z_sc = [sb.tile([P, HALF_V], U8, name="z_sc%d" % u, align_bytes=ALIGN) for u in range(2)]
+        def bounds(upper, lower, g0, g1):
+            nc.vector.tensor_tensor(upper, g0, g1, ALU.max)
+            nc.vector.tensor_tensor(lower, g0, g1, ALU.min)
 
         def woven_max(u):
             nc.vector.tensor_tensor(
                 z_bf[u][:].rearrange("p (c r t) -> p c t r", r=RUN, t=PACK),
-                capped[:, :, halves[u]].rearrange("p t (c r) -> p c t r", r=RUN),
-                lo[:, :, halves[u]].rearrange("p t (c r) -> p c t r", r=RUN),
+                capped[:, :, parts[u]].rearrange("p t (c r) -> p c t r", r=RUN),
+                lo[:, :, parts[u]].rearrange("p t (c r) -> p c t r", r=RUN),
                 ALU.max,
             )
 
-        narrow(0, 2, slice(0, V))
-        narrow(2, 3, slice(0, V))
-        for u in range(2):
-            narrow(3, 4, halves[u])
-            woven_max(u)
+        def quantise_z(u):
             nc.vector.quantize_mx(out=z_q[u][:].bitcast(FP8X4), scales=z_sc[u][:], in_=z_bf[u][:])
+
+        bounds(hi[:], lo[:, 0:2, :], g[0][:], g[1][:])
+        nc.vector.tensor_tensor(capped[:, 0:2, 0:HALF_V], hi[:, :, 0:HALF_V], g[2][:, :, 0:HALF_V], ALU.min)
+        z_first = sb.tile([P, PACK, HALF_V], BF16, name="z_first", align_bytes=ALIGN)
+        for u, part in enumerate(parts):
+            bounds(hi_late[u], lo[:, 2:4, part], g_late[u][0], g_late[u][1])
+            if u == 0:
+                nc.vector.tensor_tensor(capped[:, 2:4, part], hi_late[u], g_late[u][2], ALU.min)
+            else:
+                for t in range(2):
+                    nc.vector.tensor_tensor(capped[:, 2 + t, part], hi_late[u][:, t], g_late[u][2][:, t], ALU.min)
+            if u == 0:
+                nc.vector.tensor_tensor(capped[:, 0, HALF_V:V], hi[:, 0, HALF_V:V], g[2][:, 0, HALF_V:V], ALU.min)
+                nc.vector.tensor_tensor(z_first[:], capped[:, :, part], lo[:, :, part], ALU.max)
+                nc.vector.tensor_tensor(capped[:, 1, HALF_V:V], hi[:, 1, HALF_V:V], g2_late, ALU.min)
+                nc.scalar.copy(
+                    z_bf[0][:].rearrange("p (c r t) -> p c t r", r=RUN, t=PACK),
+                    z_first[:].rearrange("p t (c r) -> p c t r", r=RUN),
+                )
+        woven_max(1)
+        quantise_z(0)
+        quantise_z(1)
 
         def second_product(acc, u, b):
             features = slice(b * P, (b + 1) * P)
@@ -164,11 +187,13 @@ def tile_picked_ytrim_relu_p_kernel(
         out_first = psum.tile([P, 2, HALF_V], F32, name="out_first", tag="bank0")
         for b in range(2):
             second_product(out_first[:, b, :], 0, b)
-        nc.scalar.activation(res[:, :, halves[0]], out_first[:], ACT.Relu)
-        out_upper = psum.tile([P, HALF_V], F32, name="out_upper", tag="bank1")
-        second_product(out_upper[:], 1, 0)
-        nc.vector.tensor_scalar_max(res[:, 0, halves[1]], out_upper[:], 0.0)
-        out_lower = psum.tile([P, HALF_V], F32, name="out_lower", tag="bank2")
-        second_product(out_lower[:], 1, 1)
-        nc.scalar.activation(res[:, 1, halves[1]], out_lower[:], ACT.Relu)
+        nc.scalar.activation(res[:, :, parts[0]], out_first[:], ACT.Relu)
+        for u in range(1, 2):
+            for b in range(2):
+                acc = psum.tile([P, widths[u]], F32, name="acc%d%d" % (u, b), tag="bank%d" % (2 * u + b - 1))
+                second_product(acc[:], u, b)
+                if (u, b) == (1, 0):
+                    nc.vector.tensor_scalar_max(res[:, b, parts[u]], acc[:], 0.0)
+                else:
+                    nc.scalar.activation(res[:, b, parts[u]], acc[:], ACT.Relu)
         nc.sync.dma_start(out.rearrange("(p b) v -> p b v", b=2), res[:])

@@ -117,19 +117,15 @@ def tile_picked_ytrim_relu_p_kernel(
         hi = sb.tile([P, 2, V], BF16, name="hi", align_bytes=ALIGN)
         lo = sb.tile([P, PACK, V], BF16, name="lo", align_bytes=ALIGN)
         capped = sb.tile([P, PACK, V], BF16, name="capped", align_bytes=ALIGN)
-        g_rest = sb.tile([P, 6, 2, HALF_V], BF16, name="g_rest", tag="w1_q", align_bytes=ALIGN)
+        g_rest = sb.tile([P, 5, 2, HALF_V], BF16, name="g_rest", tag="w1_q", align_bytes=ALIGN)
         parts = [slice(a, b) for a, b in CUTS]
         g_late = [[capped[:, 0:2, HALF_V:V], g_rest[:, 0], g_rest[:, 1]], [g_rest[:, 2 + d] for d in range(3)]]
-        g2_late = g_rest[:, 5, 0, :]
         hi_late = [lo[:, 2:4, HALF_V:V], g_late[0][2]]
 
-        for t, d in ((0, 0), (0, 1), (1, 0), (1, 1), (0, 2)):
+        for t, d in ((0, 0), (0, 1), (1, 0), (1, 1), (0, 2), (1, 2)):
             nc.vector.tensor_copy(g[d][:, t, :], h[t][:].indirect(pos_sb[d][:]))
         lists_of = [slice(part.start // LIST_ROWS, part.stop // LIST_ROWS) for part in parts]
-        nc.vector.tensor_copy(g[2][:, 1, parts[0]], h[1][:].indirect(pos_sb[2][:, lists_of[0]]))
         for u, entries in enumerate(lists_of):
-            if u == 1:
-                nc.scalar.activation(g2_late, h[1][:].indirect(pos_sb[2][:, entries]), ACT.Copy)
             for t, d in ((2, 0), (2, 1), (3, 0), (3, 1), (2, 2), (3, 2)):
                 nc.scalar.activation(g_late[u][d][:, t - 2, :], h[t][:].indirect(pos_sb[d][:, entries]), ACT.Copy)
         nc.vector.quantize_mx(out=w2_q[:].bitcast(FP8X4), scales=w2_sc[:], in_=w2_bf[:])
@@ -165,9 +161,8 @@ def tile_picked_ytrim_relu_p_kernel(
                 for t in range(2):
                     nc.vector.tensor_tensor(capped[:, 2 + t, part], hi_late[u][:, t], g_late[u][2][:, t], ALU.min)
             if u == 0:
-                nc.vector.tensor_tensor(capped[:, 0, HALF_V:V], hi[:, 0, HALF_V:V], g[2][:, 0, HALF_V:V], ALU.min)
+                nc.vector.tensor_tensor(capped[:, 0:2, HALF_V:V], hi[:, :, HALF_V:V], g[2][:, :, HALF_V:V], ALU.min)
                 nc.vector.tensor_tensor(z_first[:], capped[:, :, part], lo[:, :, part], ALU.max)
-                nc.vector.tensor_tensor(capped[:, 1, HALF_V:V], hi[:, 1, HALF_V:V], g2_late, ALU.min)
                 nc.scalar.copy(
                     z_bf[0][:].rearrange("p (c r t) -> p c t r", r=RUN, t=PACK),
                     z_first[:].rearrange("p t (c r) -> p c t r", r=RUN),

@@ -73,7 +73,7 @@ def tile_picked_ytrim_relu_p_kernel(
         nc.vector.tensor_copy(w1_dst[:, P // 2 : P, 2:4, :], w1_src[1][:, P // 2 : P])
         nc.vector.quantize_mx(out=w1_q[:].bitcast(FP8X4), scales=w1_sc[:], in_=w1_bf[:])
 
-        x_q = sb.tile([P, S], U32, name="x_q", align_bytes=ALIGN)
+        x_q = sb.tile([P, S], U32, name="x_q", tag="x_q", align_bytes=ALIGN)
         list_cols = PIECE // LIST_ROWS
         for a in range(PIECES):
             nc.vector.tensor_copy(
@@ -90,24 +90,22 @@ def tile_picked_ytrim_relu_p_kernel(
             )
 
         h = [sb.tile([P, S], F32, name="h%d" % t) for t in range(PACK)]
-        for a in range(PIECES - 1):
+        for a in range(PIECES):
             cols = slice(a * PIECE, (a + 1) * PIECE)
-            early = psum.tile([P, 2, PIECE], F32, name="early%d" % a, tag="bank%d" % a)
-            for t in range(2):
-                first_product(early[:, t, :], t, cols)
-            for t in range(2):
-                nc.scalar.copy(h[t][:, cols], early[:, t, :])
-        for t in range(2):
-            last = psum.tile([P, PIECE], F32, name="last%d" % t, tag="bank%d" % (3 + t))
-            first_product(last[:], t, slice(S - PIECE, S))
-            nc.scalar.copy(h[t][:, S - PIECE : S], last[:])
+            piece = psum.tile([P, PIECE], F32, name="piece%d" % a, tag="bank%d" % a)
+            first_product(piece[:], 0, cols)
+            nc.scalar.copy(h[0][:, cols], piece[:])
+            if a % 2 == 1:
+                cols = slice((a - 1) * PIECE, (a + 1) * PIECE)
+                pair = psum.tile([P, 2 * PIECE], F32, name="pair%d" % a, tag="bank%d" % (4 + a // 2))
+                first_product(pair[:], 1, cols)
+                nc.scalar.copy(h[1][:, cols], pair[:])
         for t in range(2, PACK):
-            late = psum.tile([P, S], F32, name="late%d" % t, tag="bank%d" % (3 + t))
+            late = psum.tile([P, S], F32, name="late%d" % t, tag="bank%d" % (4 + t))
             first_product(late[:], t, slice(0, S))
             nc.scalar.copy(h[t][:], late[:])
 
         w2_bf = sb.tile([P, N * PACK], BF16, name="w2_bf", align_bytes=ALIGN)
-        w2_q = sb.tile([P, N], U32, name="w2_q", align_bytes=ALIGN)
         w2_sc = sb.tile([P, N], U8, name="w2_sc", align_bytes=ALIGN)
         nc.vector.tensor_copy(
             w2_bf[:].rearrange("p (b m j) -> p m j b", b=2, j=PACK), w2_raw[:].rearrange("p j (m b) -> p m j b", b=2)
@@ -117,18 +115,19 @@ def tile_picked_ytrim_relu_p_kernel(
         hi = sb.tile([P, 2, V], BF16, name="hi", align_bytes=ALIGN)
         lo = sb.tile([P, PACK, V], BF16, name="lo", align_bytes=ALIGN)
         capped = sb.tile([P, PACK, V], BF16, name="capped", align_bytes=ALIGN)
-        g_rest = sb.tile([P, 5, 2, HALF_V], BF16, name="g_rest", tag="w1_q", align_bytes=ALIGN)
+        g_rest = sb.tile([P, 3, 2, HALF_V], BF16, name="g_rest", tag="x_q", align_bytes=ALIGN)
+        g_pair = sb.tile([P, 2, 2, HALF_V], BF16, name="g_pair", tag="w1_q", align_bytes=ALIGN)
         parts = [slice(a, b) for a, b in CUTS]
-        g_late = [[capped[:, 0:2, HALF_V:V], g_rest[:, 0], g_rest[:, 1]], [g_rest[:, 2 + d] for d in range(3)]]
+        g_late = [[capped[:, 0:2, HALF_V:V], g_rest[:, 0], g_rest[:, 1]], [g_pair[:, 0], g_pair[:, 1], g_rest[:, 2]]]
         hi_late = [lo[:, 2:4, HALF_V:V], g_late[0][2]]
 
-        for t, d in ((0, 0), (0, 1), (1, 0), (1, 1), (0, 2), (1, 2)):
+        for t, d in ((0, 0), (0, 1), (0, 2), (1, 0), (1, 1)):
             nc.vector.tensor_copy(g[d][:, t, :], h[t][:].indirect(pos_sb[d][:]))
+        nc.scalar.activation(g[2][:, 1, :], h[1][:].indirect(pos_sb[2][:]), ACT.Copy)
         lists_of = [slice(part.start // LIST_ROWS, part.stop // LIST_ROWS) for part in parts]
         for u, entries in enumerate(lists_of):
             for t, d in ((2, 0), (2, 1), (3, 0), (3, 1), (2, 2), (3, 2)):
                 nc.scalar.activation(g_late[u][d][:, t - 2, :], h[t][:].indirect(pos_sb[d][:, entries]), ACT.Copy)
-        nc.vector.quantize_mx(out=w2_q[:].bitcast(FP8X4), scales=w2_sc[:], in_=w2_bf[:])
 
         widths = [part.stop - part.start for part in parts]
         z_bf = [sb.tile([P, w * PACK], BF16, name="z_bf%d" % u, align_bytes=ALIGN) for u, w in enumerate(widths)]
@@ -167,6 +166,8 @@ def tile_picked_ytrim_relu_p_kernel(
                     z_bf[0][:].rearrange("p (c r t) -> p c t r", r=RUN, t=PACK),
                     z_first[:].rearrange("p t (c r) -> p c t r", r=RUN),
                 )
+        w2_q = sb.tile([P, N], U32, name="w2_q", tag="w1_q", align_bytes=ALIGN)
+        nc.vector.quantize_mx(out=w2_q[:].bitcast(FP8X4), scales=w2_sc[:], in_=w2_bf[:])
         woven_max(1)
         quantise_z(0)
         quantise_z(1)

@@ -22,7 +22,6 @@ QUADRANT = 32
 PIECE = 128
 PIECES = S // PIECE
 HALF_V = V // 2
-CUTS = ((0, 128), (128, 256))
 RUN = 4
 ALIGN = 64
 GPSIMD_CLEARS = 128
@@ -65,7 +64,7 @@ def tile_picked_ytrim_relu_p_kernel(
 
         w1_bf = sb.tile([P, H * PACK], BF16, name="w1_bf", align_bytes=ALIGN)
         w1_q = sb.tile([P, H], U32, name="w1_q", tag="w1_q", align_bytes=ALIGN)
-        w1_sc = sb.tile([P, H], U8, name="w1_sc", align_bytes=ALIGN)
+        w1_sc = sb.tile([P, H], U8, name="w1_sc", tag="w1_sc", align_bytes=ALIGN)
         w1_dst = w1_bf[:].rearrange("p (t m j) -> p m j t", t=PACK, j=PACK)
         w1_src = [w1_raw[a][:].rearrange("p j (m t) -> p m j t", t=PACK) for a in range(2)]
         nc.scalar.copy(w1_dst[:, :, 0:2, :], w1_src[0])
@@ -106,76 +105,84 @@ def tile_picked_ytrim_relu_p_kernel(
             nc.scalar.copy(h[t][:], late[:])
 
         w2_bf = sb.tile([P, N * PACK], BF16, name="w2_bf", align_bytes=ALIGN)
-        w2_sc = sb.tile([P, N], U8, name="w2_sc", align_bytes=ALIGN)
         nc.vector.tensor_copy(
             w2_bf[:].rearrange("p (b m j) -> p m j b", b=2, j=PACK), w2_raw[:].rearrange("p j (m b) -> p m j b", b=2)
         )
 
-        g = [sb.tile([P, 2, V], BF16, name="g%d" % d, align_bytes=ALIGN) for d in range(3)]
-        hi = sb.tile([P, 2, V], BF16, name="hi", align_bytes=ALIGN)
-        lo = sb.tile([P, PACK, V], BF16, name="lo", align_bytes=ALIGN)
-        capped = sb.tile([P, PACK, V], BF16, name="capped", align_bytes=ALIGN)
-        g_rest = sb.tile([P, 3, 2, HALF_V], BF16, name="g_rest", tag="x_q", align_bytes=ALIGN)
-        g_pair = sb.tile([P, 2, 2, HALF_V], BF16, name="g_pair", tag="w1_q", align_bytes=ALIGN)
-        parts = [slice(a, b) for a, b in CUTS]
-        g_late = [[capped[:, 0:2, HALF_V:V], g_rest[:, 0], g_rest[:, 1]], [g_pair[:, 0], g_pair[:, 1], g_rest[:, 2]]]
-        hi_late = [lo[:, 2:4, HALF_V:V], g_late[0][2]]
+        halves = [slice(u * HALF_V, (u + 1) * HALF_V) for u in range(2)]
+        entries = [slice(half.start // LIST_ROWS, half.stop // LIST_ROWS) for half in halves]
+        w2_q = [None, None]
+        w2_sc = [sb.tile([P, P], U8, name="w2_sc%d" % b, align_bytes=ALIGN) for b in range(2)]
 
-        for t, d in ((0, 0), (0, 1), (0, 2), (1, 0), (1, 1)):
-            nc.vector.tensor_copy(g[d][:, t, :], h[t][:].indirect(pos_sb[d][:]))
-        nc.scalar.activation(g[2][:, 1, :], h[1][:].indirect(pos_sb[2][:]), ACT.Copy)
-        lists_of = [slice(part.start // LIST_ROWS, part.stop // LIST_ROWS) for part in parts]
-        for u, entries in enumerate(lists_of):
-            for t, d in ((2, 0), (2, 1), (3, 0), (3, 1), (2, 2), (3, 2)):
-                nc.scalar.activation(g_late[u][d][:, t - 2, :], h[t][:].indirect(pos_sb[d][:, entries]), ACT.Copy)
-
-        widths = [part.stop - part.start for part in parts]
-        z_bf = [sb.tile([P, w * PACK], BF16, name="z_bf%d" % u, align_bytes=ALIGN) for u, w in enumerate(widths)]
-        z_q = [sb.tile([P, w], U32, name="z_q%d" % u, align_bytes=ALIGN) for u, w in enumerate(widths)]
-        z_sc = [sb.tile([P, w], U8, name="z_sc%d" % u, align_bytes=ALIGN) for u, w in enumerate(widths)]
-
-        def bounds(upper, lower, g0, g1):
-            nc.vector.tensor_tensor(upper, g0, g1, ALU.max)
-            nc.vector.tensor_tensor(lower, g0, g1, ALU.min)
-
-        def woven_max(u):
-            nc.vector.tensor_tensor(
-                z_bf[u][:].rearrange("p (c r t) -> p c t r", r=RUN, t=PACK),
-                capped[:, :, parts[u]].rearrange("p t (c r) -> p c t r", r=RUN),
-                lo[:, :, parts[u]].rearrange("p t (c r) -> p c t r", r=RUN),
-                ALU.max,
+        def quantise_w2(b, tag):
+            w2_q[b] = sb.tile([P, P], U32, name="w2_q%d" % b, tag=tag, align_bytes=ALIGN)
+            nc.vector.quantize_mx(
+                out=w2_q[b][:].bitcast(FP8X4), scales=w2_sc[b][:], in_=w2_bf[:, b * P * PACK : (b + 1) * P * PACK]
             )
 
-        def quantise_z(u):
+        quantise_w2(0, "w2_q0")
+
+        g01 = [sb.tile([P, 2, V], BF16, name="g%d" % d, align_bytes=ALIGN) for d in range(2)]
+        shelf = sb.tile([P, 14, HALF_V], BF16, name="shelf", align_bytes=ALIGN)
+        g2_first = shelf[:, 2:6, :]
+        hi = sb.tile([P, PACK, V], BF16, name="hi", align_bytes=ALIGN)
+        lo = sb.tile([P, PACK, V], BF16, name="lo", align_bytes=ALIGN)
+        capped_first = sb.tile([P, PACK, HALF_V], BF16, name="capped_first", align_bytes=ALIGN)
+        capped = [capped_first[:], shelf[:, 1:5, :]]
+        g0_late = shelf[:].rearrange("p (t a) v -> p t (a v)", t=2)[:, :, 0:V]
+        g1_late = sb.tile([P, 2, V], BF16, name="g1_late", tag="w1_q", align_bytes=ALIGN)
+        g2_mid = sb.tile([P, 2, HALF_V], BF16, name="g2_mid", tag="x_q", align_bytes=ALIGN)
+        g2_last = sb.tile([P, HALF_V], BF16, name="g2_last", tag="w1_sc", align_bytes=ALIGN)
+
+        def fetch_on_vector(dst, t, offsets):
+            nc.vector.tensor_copy(dst, h[t][:].indirect(offsets))
+
+        def fetch_on_scalar(dst, t, offsets):
+            nc.scalar.activation(dst, h[t][:].indirect(offsets), ACT.Copy)
+
+        for d in range(2):
+            fetch_on_vector(g01[d][:, 0, :], 0, pos_sb[d][:])
+        fetch_on_vector(shelf[:, 2:7:4, :], 0, pos_sb[2][:])
+        for d in range(2):
+            fetch_on_vector(g01[d][:, 1, :], 1, pos_sb[d][:])
+        fetch_on_vector(g2_first[:, 1, :], 1, pos_sb[2][:, entries[0]])
+        for t in range(2, PACK):
+            fetch_on_scalar(g0_late[:, t - 2, :], t, pos_sb[0][:])
+            fetch_on_scalar(g1_late[:, t - 2, :], t, pos_sb[1][:])
+        for t in range(2, PACK):
+            fetch_on_scalar(g2_first[:, t, :], t, pos_sb[2][:, entries[0]])
+        for t in range(1, 3):
+            fetch_on_scalar(g2_mid[:, t - 1, :], t, pos_sb[2][:, entries[1]])
+        fetch_on_scalar(g2_last[:], 3, pos_sb[2][:, entries[1]])
+
+        z_first = sb.tile([P, PACK, HALF_V], BF16, name="z_first", align_bytes=ALIGN)
+        z_bf = [sb.tile([P, HALF_V * PACK], BF16, name="z_bf%d" % u, align_bytes=ALIGN) for u in range(2)]
+        z_q = [sb.tile([P, HALF_V], U32, name="z_q%d" % u, align_bytes=ALIGN) for u in range(2)]
+        z_sc = [sb.tile([P, HALF_V], U8, name="z_sc%d" % u, align_bytes=ALIGN) for u in range(2)]
+
+        def woven(ap):
+            return ap.rearrange("p (c r t) -> p c t r", r=RUN, t=PACK)
+
+        def in_runs(ap):
+            return ap.rearrange("p t (c r) -> p c t r", r=RUN)
+
+        for tiles, g0, g1 in ((slice(0, 2), g01[0][:], g01[1][:]), (slice(2, 4), g0_late, g1_late[:])):
+            nc.vector.tensor_tensor(hi[:, tiles, :], g0, g1, ALU.max)
+            nc.vector.tensor_tensor(lo[:, tiles, :], g0, g1, ALU.min)
+        nc.vector.tensor_tensor(capped[0], hi[:, :, halves[0]], g2_first, ALU.min)
+        nc.vector.tensor_tensor(capped[1][:, 0, :], hi[:, 0, halves[1]], shelf[:, 6, :], ALU.min)
+        nc.vector.tensor_tensor(z_first[:], capped[0], lo[:, :, halves[0]], ALU.max)
+        nc.scalar.copy(woven(z_bf[0][:]), in_runs(z_first[:]))
+        nc.vector.tensor_tensor(capped[1][:, 1:3, :], hi[:, 1:3, halves[1]], g2_mid[:], ALU.min)
+        nc.vector.tensor_tensor(capped[1][:, 3, :], hi[:, 3, halves[1]], g2_last[:], ALU.min)
+        quantise_w2(1, "x_q")
+        nc.vector.tensor_tensor(woven(z_bf[1][:]), in_runs(capped[1]), in_runs(lo[:, :, halves[1]]), ALU.max)
+        for u in range(2):
             nc.vector.quantize_mx(out=z_q[u][:].bitcast(FP8X4), scales=z_sc[u][:], in_=z_bf[u][:])
 
-        bounds(hi[:], lo[:, 0:2, :], g[0][:], g[1][:])
-        nc.vector.tensor_tensor(capped[:, 0:2, 0:HALF_V], hi[:, :, 0:HALF_V], g[2][:, :, 0:HALF_V], ALU.min)
-        z_first = sb.tile([P, PACK, HALF_V], BF16, name="z_first", align_bytes=ALIGN)
-        for u, part in enumerate(parts):
-            bounds(hi_late[u], lo[:, 2:4, part], g_late[u][0], g_late[u][1])
-            if u == 0:
-                nc.vector.tensor_tensor(capped[:, 2:4, part], hi_late[u], g_late[u][2], ALU.min)
-            else:
-                for t in range(2):
-                    nc.vector.tensor_tensor(capped[:, 2 + t, part], hi_late[u][:, t], g_late[u][2][:, t], ALU.min)
-            if u == 0:
-                nc.vector.tensor_tensor(capped[:, 0:2, HALF_V:V], hi[:, :, HALF_V:V], g[2][:, :, HALF_V:V], ALU.min)
-                nc.vector.tensor_tensor(z_first[:], capped[:, :, part], lo[:, :, part], ALU.max)
-                nc.scalar.copy(
-                    z_bf[0][:].rearrange("p (c r t) -> p c t r", r=RUN, t=PACK),
-                    z_first[:].rearrange("p t (c r) -> p c t r", r=RUN),
-                )
-        w2_q = sb.tile([P, N], U32, name="w2_q", tag="w1_q", align_bytes=ALIGN)
-        nc.vector.quantize_mx(out=w2_q[:].bitcast(FP8X4), scales=w2_sc[:], in_=w2_bf[:])
-        woven_max(1)
-        quantise_z(0)
-        quantise_z(1)
-
         def second_product(acc, u, b):
-            features = slice(b * P, (b + 1) * P)
             nc.tensor.matmul_mx(
-                out=acc, lhsT=w2_q[:, features].bitcast(FP8X4), lhsT_scale=w2_sc[:, features],
+                out=acc, lhsT=w2_q[b][:].bitcast(FP8X4), lhsT_scale=w2_sc[b][:],
                 rhs=z_q[u][:].bitcast(FP8X4), rhs_scale=z_sc[u][:], start=True, stop=True,
             )
 
@@ -183,13 +190,11 @@ def tile_picked_ytrim_relu_p_kernel(
         out_first = psum.tile([P, 2, HALF_V], F32, name="out_first", tag="bank0")
         for b in range(2):
             second_product(out_first[:, b, :], 0, b)
-        nc.scalar.activation(res[:, :, parts[0]], out_first[:], ACT.Relu)
-        for u in range(1, 2):
-            for b in range(2):
-                acc = psum.tile([P, widths[u]], F32, name="acc%d%d" % (u, b), tag="bank%d" % (2 * u + b - 1))
-                second_product(acc[:], u, b)
-                if (u, b) == (1, 0):
-                    nc.vector.tensor_scalar_max(res[:, b, parts[u]], acc[:], 0.0)
-                else:
-                    nc.scalar.activation(res[:, b, parts[u]], acc[:], ACT.Relu)
+        nc.scalar.activation(res[:, :, halves[0]], out_first[:], ACT.Relu)
+        out_upper = psum.tile([P, HALF_V], F32, name="out_upper", tag="bank1")
+        second_product(out_upper[:], 1, 0)
+        nc.vector.tensor_scalar_max(res[:, 0, halves[1]], out_upper[:], 0.0)
+        out_lower = psum.tile([P, HALF_V], F32, name="out_lower", tag="bank2")
+        second_product(out_lower[:], 1, 1)
+        nc.scalar.activation(res[:, 1, halves[1]], out_lower[:], ACT.Relu)
         nc.sync.dma_start(out.rearrange("(p b) v -> p b v", b=2), res[:])

@@ -23,6 +23,7 @@ PIECE = 128
 PIECES = S // PIECE
 HALF_V = V // 2
 RUN = 4
+SPREAD = 8
 ALIGN = 64
 GPSIMD_CLEARS = 128
 
@@ -39,37 +40,48 @@ def tile_picked_ytrim_relu_p_kernel(
         offs_sb = lists.tile([P, S // LIST_ROWS], U16, name="offs_sb")
         pos_sb = [lists.tile([P, V // LIST_ROWS], U16, name="pos_sb%d" % d) for d in range(3)]
 
-        scale_win = sb.tile([P, T], U8, name="scale_win", align_bytes=ALIGN)
+        scale_win = sb.tile([P, T], U8, name="scale_win", tag="scale_win", align_bytes=ALIGN)
         word_win = sb.tile([P, T], I32, name="word_win", align_bytes=ALIGN)
-        w1_raw = [sb.tile([P, 2, H], F32, name="w1_raw%d" % a, align_bytes=ALIGN) for a in range(2)]
-        w2_raw = sb.tile([P, PACK, N], F32, name="w2_raw", align_bytes=ALIGN)
+        w1_first = [sb.tile([P, 2, H // 2], F32, name="w1_first%d" % a, align_bytes=ALIGN) for a in range(2)]
+        w1_second = sb.tile([P, 2, H], F32, name="w1_second", align_bytes=ALIGN)
+        x_sc = sb.tile([P, S], U8, name="x_sc", align_bytes=ALIGN)
 
         nc.gpsimd.memset(scale_win[:].bitcast(I32)[:, 0:GPSIMD_CLEARS], 0)
         nc.vector.memset(scale_win[:].bitcast(I32)[:, GPSIMD_CLEARS : T // 4], 0)
+        nc.gpsimd.memset(x_sc[:].bitcast(I32), 0)
 
         w1_rows = w1.rearrange("(p j) c -> p j c", j=PACK)
-        nc.sync.dma_start(w1_raw[0][:], w1_rows[:, 0:2, :])
+        w2_rows = w2.rearrange("(p j) n -> p j n", j=PACK)
+        nc.sync.dma_start(w1_first[0][:], w1_rows[:, 0:2, 0 : H // 2])
         nc.sync.dma_start(offs_sb[:], offs)
-        scale_rows = x_scales[0].rearrange("(q r) c -> r q c", r=4)
-        for r in range(4):
-            nc.sync.dma_start(scale_win[r:P:QUADRANT, :].bitcast(I32), scale_rows[r].bitcast(I32))
-        nc.sync.dma_start(w1_raw[1][:], w1_rows[:, 2:4, :])
+        nc.sync.dma_start(scale_win[0:P:SPREAD, :].bitcast(I32), x_scales[0].bitcast(I32))
+        nc.sync.dma_start(w1_first[1][:], w1_rows[:, 0:2, H // 2 : H])
+        nc.sync.dma_start(pos_sb[0][:], pos1)
+        nc.sync.dma_start(pos_sb[1][:], pos2)
+        nc.sync.dma_start(w1_second[:], w1_rows[:, 2:4, :])
         nc.sync.dma_start(word_win[:], x_words[0].rearrange("p n t -> p (n t)").bitcast(I32))
-        nc.sync.dma_start(w2_raw[:], w2.rearrange("(p j) n -> p j n", j=PACK))
-        for d, pos in enumerate((pos1, pos2, pos3)):
-            nc.sync.dma_start(pos_sb[d][:], pos)
+        w2_early = sb.tile([P, 2, N], F32, name="w2_early", align_bytes=ALIGN)
+        nc.sync.dma_start(w2_early[:], w2_rows[:, 0:2, :])
+        nc.sync.dma_start(pos_sb[2][:], pos3)
 
-        x_sc = sb.tile([P, S], U8, name="x_sc", align_bytes=ALIGN)
-        nc.vector.tensor_copy(x_sc[:], scale_win[:].indirect(offs_sb[:]))
+        sc_spread = sb.tile([P, S], U8, name="sc_spread", align_bytes=ALIGN)
+        nc.vector.tensor_copy(sc_spread[:], scale_win[:].indirect(offs_sb[:]))
+        for r in range(4):
+            nc.sync.dma_start(x_sc[r:P:QUADRANT, :].bitcast(I32), sc_spread[r * SPREAD : P : QUADRANT, :].bitcast(I32))
+        w2_late = sb.tile([P, 2, N], F32, name="w2_late", tag="scale_win", align_bytes=ALIGN)
+        nc.sync.dma_start(w2_late[:], w2_rows[:, 2:4, :])
 
         w1_bf = sb.tile([P, H * PACK], BF16, name="w1_bf", align_bytes=ALIGN)
         w1_q = sb.tile([P, H], U32, name="w1_q", tag="w1_q", align_bytes=ALIGN)
         w1_sc = sb.tile([P, H], U8, name="w1_sc", tag="w1_sc", align_bytes=ALIGN)
         w1_dst = w1_bf[:].rearrange("p (t m j) -> p m j t", t=PACK, j=PACK)
-        w1_src = [w1_raw[a][:].rearrange("p j (m t) -> p m j t", t=PACK) for a in range(2)]
-        nc.scalar.copy(w1_dst[:, :, 0:2, :], w1_src[0])
-        nc.scalar.copy(w1_dst[:, 0 : P // 2, 2:4, :], w1_src[1][:, 0 : P // 2])
-        nc.vector.tensor_copy(w1_dst[:, P // 2 : P, 2:4, :], w1_src[1][:, P // 2 : P])
+        for a in range(2):
+            nc.scalar.copy(
+                w1_dst[:, a * P // 2 : (a + 1) * P // 2, 0:2, :], w1_first[a][:].rearrange("p j (m t) -> p m j t", t=PACK)
+            )
+        w1_src = w1_second[:].rearrange("p j (m t) -> p m j t", t=PACK)
+        nc.scalar.copy(w1_dst[:, 0 : P // 2, 2:4, :], w1_src[:, 0 : P // 2])
+        nc.vector.tensor_copy(w1_dst[:, P // 2 : P, 2:4, :], w1_src[:, P // 2 : P])
         nc.vector.quantize_mx(out=w1_q[:].bitcast(FP8X4), scales=w1_sc[:], in_=w1_bf[:])
 
         x_q = sb.tile([P, S], U32, name="x_q", tag="x_q", align_bytes=ALIGN)
@@ -105,9 +117,9 @@ def tile_picked_ytrim_relu_p_kernel(
             nc.scalar.copy(h[t][:], late[:])
 
         w2_bf = sb.tile([P, N * PACK], BF16, name="w2_bf", align_bytes=ALIGN)
-        nc.vector.tensor_copy(
-            w2_bf[:].rearrange("p (b m j) -> p m j b", b=2, j=PACK), w2_raw[:].rearrange("p j (m b) -> p m j b", b=2)
-        )
+        w2_dst = w2_bf[:].rearrange("p (b m j) -> p m j b", b=2, j=PACK)
+        for a, raw in enumerate((w2_early, w2_late)):
+            nc.vector.tensor_copy(w2_dst[:, :, 2 * a : 2 * a + 2, :], raw[:].rearrange("p j (m b) -> p m j b", b=2))
 
         halves = [slice(u * HALF_V, (u + 1) * HALF_V) for u in range(2)]
         entries = [slice(half.start // LIST_ROWS, half.stop // LIST_ROWS) for half in halves]

@@ -24,8 +24,9 @@ PIECES = S // PIECE
 HALF_V = V // 2
 RUN = 4
 SPREAD = 8
+LEAD = 320
+SCALAR_DEALS = 40
 ALIGN = 64
-GPSIMD_CLEARS = 128
 
 
 def tile_picked_ytrim_relu_p_kernel(
@@ -42,46 +43,45 @@ def tile_picked_ytrim_relu_p_kernel(
 
         scale_win = sb.tile([P, T], U8, name="scale_win", tag="scale_win", align_bytes=ALIGN)
         word_win = sb.tile([P, T], I32, name="word_win", align_bytes=ALIGN)
-        w1_first = [sb.tile([P, 2, H // 2], F32, name="w1_first%d" % a, align_bytes=ALIGN) for a in range(2)]
+        w1_lead = sb.tile([P, 2, LEAD], F32, name="w1_lead", align_bytes=ALIGN)
+        w2_raw = sb.tile([P, PACK, N], F32, name="w2_raw", align_bytes=ALIGN)
+        w1_first = [w1_lead[:], w2_raw[:, 2:4, 0 : H - LEAD]]
         w1_second = sb.tile([P, 2, H], F32, name="w1_second", align_bytes=ALIGN)
         x_sc = sb.tile([P, S], U8, name="x_sc", align_bytes=ALIGN)
 
-        nc.gpsimd.memset(scale_win[:].bitcast(I32)[:, 0:GPSIMD_CLEARS], 0)
-        nc.vector.memset(scale_win[:].bitcast(I32)[:, GPSIMD_CLEARS : T // 4], 0)
-        nc.gpsimd.memset(x_sc[:].bitcast(I32), 0)
+        nc.vector.memset(scale_win[:].bitcast(I32), 0)
+        nc.vector.memset(x_sc[:].bitcast(I32), 0)
 
         w1_rows = w1.rearrange("(p j) c -> p j c", j=PACK)
         w2_rows = w2.rearrange("(p j) n -> p j n", j=PACK)
-        nc.sync.dma_start(w1_first[0][:], w1_rows[:, 0:2, 0 : H // 2])
+        nc.sync.dma_start(w1_first[0], w1_rows[:, 0:2, 0:LEAD])
         nc.sync.dma_start(offs_sb[:], offs)
-        nc.sync.dma_start(scale_win[0:P:SPREAD, :].bitcast(I32), x_scales[0].bitcast(I32))
-        nc.sync.dma_start(w1_first[1][:], w1_rows[:, 0:2, H // 2 : H])
         nc.sync.dma_start(pos_sb[0][:], pos1)
+        nc.sync.dma_start(scale_win[0:P:SPREAD, :].bitcast(I32), x_scales[0].bitcast(I32))
+        nc.sync.dma_start(w1_first[1], w1_rows[:, 0:2, LEAD:H])
         nc.sync.dma_start(pos_sb[1][:], pos2)
         nc.sync.dma_start(w1_second[:], w1_rows[:, 2:4, :])
         nc.sync.dma_start(word_win[:], x_words[0].rearrange("p n t -> p (n t)").bitcast(I32))
-        w2_early = sb.tile([P, 2, N], F32, name="w2_early", align_bytes=ALIGN)
-        nc.sync.dma_start(w2_early[:], w2_rows[:, 0:2, :])
+        nc.sync.dma_start(w2_raw[:, 0:2, :], w2_rows[:, 0:2, :])
         nc.sync.dma_start(pos_sb[2][:], pos3)
 
         sc_spread = sb.tile([P, S], U8, name="sc_spread", align_bytes=ALIGN)
         nc.vector.tensor_copy(sc_spread[:], scale_win[:].indirect(offs_sb[:]))
         for r in range(4):
             nc.sync.dma_start(x_sc[r:P:QUADRANT, :].bitcast(I32), sc_spread[r * SPREAD : P : QUADRANT, :].bitcast(I32))
-        w2_late = sb.tile([P, 2, N], F32, name="w2_late", tag="scale_win", align_bytes=ALIGN)
-        nc.sync.dma_start(w2_late[:], w2_rows[:, 2:4, :])
 
         w1_bf = sb.tile([P, H * PACK], BF16, name="w1_bf", align_bytes=ALIGN)
         w1_q = sb.tile([P, H], U32, name="w1_q", tag="w1_q", align_bytes=ALIGN)
         w1_sc = sb.tile([P, H], U8, name="w1_sc", tag="w1_sc", align_bytes=ALIGN)
         w1_dst = w1_bf[:].rearrange("p (t m j) -> p m j t", t=PACK, j=PACK)
-        for a in range(2):
-            nc.scalar.copy(
-                w1_dst[:, a * P // 2 : (a + 1) * P // 2, 0:2, :], w1_first[a][:].rearrange("p j (m t) -> p m j t", t=PACK)
-            )
+        first_src = [w1_first[a].rearrange("p j (m t) -> p m j t", t=PACK) for a in range(2)]
+        nc.scalar.copy(w1_dst[:, 0:80, 0:2, :], first_src[0])
+        nc.scalar.copy(w1_dst[:, 80:96, 0:2, :], first_src[1][:, 0:16])
+        nc.vector.tensor_copy(w1_dst[:, 96:128, 0:2, :], first_src[1][:, 16:48])
+        nc.sync.dma_start(w2_raw[:, 2:4, :], w2_rows[:, 2:4, :])
         w1_src = w1_second[:].rearrange("p j (m t) -> p m j t", t=PACK)
-        nc.scalar.copy(w1_dst[:, 0 : P // 2, 2:4, :], w1_src[:, 0 : P // 2])
-        nc.vector.tensor_copy(w1_dst[:, P // 2 : P, 2:4, :], w1_src[:, P // 2 : P])
+        nc.scalar.copy(w1_dst[:, 0:SCALAR_DEALS, 2:4, :], w1_src[:, 0:SCALAR_DEALS])
+        nc.vector.tensor_copy(w1_dst[:, SCALAR_DEALS:P, 2:4, :], w1_src[:, SCALAR_DEALS:P])
         nc.vector.quantize_mx(out=w1_q[:].bitcast(FP8X4), scales=w1_sc[:], in_=w1_bf[:])
 
         x_q = sb.tile([P, S], U32, name="x_q", tag="x_q", align_bytes=ALIGN)
@@ -117,9 +117,10 @@ def tile_picked_ytrim_relu_p_kernel(
             nc.scalar.copy(h[t][:], late[:])
 
         w2_bf = sb.tile([P, N * PACK], BF16, name="w2_bf", align_bytes=ALIGN)
-        w2_dst = w2_bf[:].rearrange("p (b m j) -> p m j b", b=2, j=PACK)
-        for a, raw in enumerate((w2_early, w2_late)):
-            nc.vector.tensor_copy(w2_dst[:, :, 2 * a : 2 * a + 2, :], raw[:].rearrange("p j (m b) -> p m j b", b=2))
+        w2_dst = w2_bf[:].rearrange("p (b m j) -> p b m j", b=2, j=PACK)
+        w2_src = w2_raw[:].rearrange("p j (m b) -> p b m j", b=2)
+        for b in range(2):
+            nc.vector.tensor_copy(w2_dst[:, b], w2_src[:, b])
 
         halves = [slice(u * HALF_V, (u + 1) * HALF_V) for u in range(2)]
         entries = [slice(half.start // LIST_ROWS, half.stop // LIST_ROWS) for half in halves]

@@ -24,8 +24,7 @@ PIECES = S // PIECE
 HALF_V = V // 2
 RUN = 4
 SPREAD = 8
-LEAD = 320
-SCALAR_DEALS = 40
+SCALAR_DEALS = 32
 ALIGN = 64
 
 
@@ -43,10 +42,10 @@ def tile_picked_ytrim_relu_p_kernel(
 
         scale_win = sb.tile([P, T], U8, name="scale_win", tag="scale_win", align_bytes=ALIGN)
         word_win = sb.tile([P, T], I32, name="word_win", align_bytes=ALIGN)
-        w1_lead = sb.tile([P, 2, LEAD], F32, name="w1_lead", align_bytes=ALIGN)
-        w2_raw = sb.tile([P, PACK, N], F32, name="w2_raw", align_bytes=ALIGN)
-        w1_first = [w1_lead[:], w2_raw[:, 2:4, 0 : H - LEAD]]
+        stage = sb.tile([P, 3 * H], F32, name="stage", align_bytes=ALIGN)
         w1_second = sb.tile([P, 2, H], F32, name="w1_second", align_bytes=ALIGN)
+        w1_raw = [stage[:, H : 3 * H].rearrange("p (j c) -> p j c", j=2), w1_second[:]]
+        w2_raw = stage[:, 0 : PACK * N].rearrange("p (j n) -> p j n", j=PACK)
         x_sc = sb.tile([P, S], U8, name="x_sc", align_bytes=ALIGN)
 
         nc.vector.memset(scale_win[:].bitcast(I32), 0)
@@ -54,13 +53,12 @@ def tile_picked_ytrim_relu_p_kernel(
 
         w1_rows = w1.rearrange("(p j) c -> p j c", j=PACK)
         w2_rows = w2.rearrange("(p j) n -> p j n", j=PACK)
-        nc.sync.dma_start(w1_first[0], w1_rows[:, 0:2, 0:LEAD])
+        nc.sync.dma_start(w1_raw[0], w1_rows[:, 0:2, :])
         nc.sync.dma_start(offs_sb[:], offs)
         nc.sync.dma_start(pos_sb[0][:], pos1)
         nc.sync.dma_start(scale_win[0:P:SPREAD, :].bitcast(I32), x_scales[0].bitcast(I32))
-        nc.sync.dma_start(w1_first[1], w1_rows[:, 0:2, LEAD:H])
         nc.sync.dma_start(pos_sb[1][:], pos2)
-        nc.sync.dma_start(w1_second[:], w1_rows[:, 2:4, :])
+        nc.sync.dma_start(w1_raw[1], w1_rows[:, 2:4, :])
         nc.sync.dma_start(word_win[:], x_words[0].rearrange("p n t -> p (n t)").bitcast(I32))
         nc.sync.dma_start(w2_raw[:, 0:2, :], w2_rows[:, 0:2, :])
         nc.sync.dma_start(pos_sb[2][:], pos3)
@@ -74,14 +72,11 @@ def tile_picked_ytrim_relu_p_kernel(
         w1_q = sb.tile([P, H], U32, name="w1_q", tag="w1_q", align_bytes=ALIGN)
         w1_sc = sb.tile([P, H], U8, name="w1_sc", tag="w1_sc", align_bytes=ALIGN)
         w1_dst = w1_bf[:].rearrange("p (t m j) -> p m j t", t=PACK, j=PACK)
-        first_src = [w1_first[a].rearrange("p j (m t) -> p m j t", t=PACK) for a in range(2)]
-        nc.scalar.copy(w1_dst[:, 0:80, 0:2, :], first_src[0])
-        nc.scalar.copy(w1_dst[:, 80:96, 0:2, :], first_src[1][:, 0:16])
-        nc.vector.tensor_copy(w1_dst[:, 96:128, 0:2, :], first_src[1][:, 16:48])
+        w1_src = [w1_raw[a].rearrange("p j (m t) -> p m j t", t=PACK) for a in range(2)]
+        nc.scalar.copy(w1_dst[:, :, 0:2, :], w1_src[0])
         nc.sync.dma_start(w2_raw[:, 2:4, :], w2_rows[:, 2:4, :])
-        w1_src = w1_second[:].rearrange("p j (m t) -> p m j t", t=PACK)
-        nc.scalar.copy(w1_dst[:, 0:SCALAR_DEALS, 2:4, :], w1_src[:, 0:SCALAR_DEALS])
-        nc.vector.tensor_copy(w1_dst[:, SCALAR_DEALS:P, 2:4, :], w1_src[:, SCALAR_DEALS:P])
+        nc.scalar.copy(w1_dst[:, 0:SCALAR_DEALS, 2:4, :], w1_src[1][:, 0:SCALAR_DEALS])
+        nc.vector.tensor_copy(w1_dst[:, SCALAR_DEALS:P, 2:4, :], w1_src[1][:, SCALAR_DEALS:P])
         nc.vector.quantize_mx(out=w1_q[:].bitcast(FP8X4), scales=w1_sc[:], in_=w1_bf[:])
 
         x_q = sb.tile([P, S], U32, name="x_q", tag="x_q", align_bytes=ALIGN)
@@ -111,6 +106,8 @@ def tile_picked_ytrim_relu_p_kernel(
                 pair = psum.tile([P, 2 * PIECE], F32, name="pair%d" % a, tag="bank%d" % (4 + a // 2))
                 first_product(pair[:], 1, cols)
                 nc.scalar.copy(h[1][:, cols], pair[:])
+        g01 = [sb.tile([P, 2, V], BF16, name="g%d" % d, align_bytes=ALIGN) for d in range(2)]
+        nc.scalar.activation(g01[1][:, 0, :], h[0][:].indirect(pos_sb[1][:]), ACT.Copy)
         for t in range(2, PACK):
             late = psum.tile([P, S], F32, name="late%d" % t, tag="bank%d" % (4 + t))
             first_product(late[:], t, slice(0, S))
@@ -118,7 +115,7 @@ def tile_picked_ytrim_relu_p_kernel(
 
         w2_bf = sb.tile([P, N * PACK], BF16, name="w2_bf", align_bytes=ALIGN)
         w2_dst = w2_bf[:].rearrange("p (b m j) -> p b m j", b=2, j=PACK)
-        w2_src = w2_raw[:].rearrange("p j (m b) -> p b m j", b=2)
+        w2_src = w2_raw.rearrange("p j (m b) -> p b m j", b=2)
         for b in range(2):
             nc.vector.tensor_copy(w2_dst[:, b], w2_src[:, b])
 
@@ -135,7 +132,6 @@ def tile_picked_ytrim_relu_p_kernel(
 
         quantise_w2(0, "w2_q0")
 
-        g01 = [sb.tile([P, 2, V], BF16, name="g%d" % d, align_bytes=ALIGN) for d in range(2)]
         shelf = sb.tile([P, 14, HALF_V], BF16, name="shelf", align_bytes=ALIGN)
         g2_first = shelf[:, 2:6, :]
         hi = sb.tile([P, PACK, V], BF16, name="hi", align_bytes=ALIGN)
@@ -153,15 +149,15 @@ def tile_picked_ytrim_relu_p_kernel(
         def fetch_on_scalar(dst, t, offsets):
             nc.scalar.activation(dst, h[t][:].indirect(offsets), ACT.Copy)
 
-        for d in range(2):
-            fetch_on_vector(g01[d][:, 0, :], 0, pos_sb[d][:])
+        fetch_on_vector(g01[0][:, 0, :], 0, pos_sb[0][:])
         fetch_on_vector(shelf[:, 2:7:4, :], 0, pos_sb[2][:])
         for d in range(2):
             fetch_on_vector(g01[d][:, 1, :], 1, pos_sb[d][:])
         fetch_on_vector(g2_first[:, 1, :], 1, pos_sb[2][:, entries[0]])
-        for t in range(2, PACK):
-            fetch_on_scalar(g0_late[:, t - 2, :], t, pos_sb[0][:])
-            fetch_on_scalar(g1_late[:, t - 2, :], t, pos_sb[1][:])
+        fetch_on_vector(g0_late[:, 0, :], 2, pos_sb[0][:])
+        fetch_on_scalar(g1_late[:, 0, :], 2, pos_sb[1][:])
+        fetch_on_scalar(g0_late[:, 1, :], 3, pos_sb[0][:])
+        fetch_on_scalar(g1_late[:, 1, :], 3, pos_sb[1][:])
         for t in range(2, PACK):
             fetch_on_scalar(g2_first[:, t, :], t, pos_sb[2][:, entries[0]])
         for t in range(1, 3):

@@ -24,7 +24,8 @@ PIECES = S // PIECE
 HALF_V = V // 2
 RUN = 4
 SPREAD = 8
-SCALAR_DEALS = 32
+VECTOR_DEALS = 72
+SHARED = 32
 ALIGN = 64
 
 
@@ -42,10 +43,9 @@ def tile_picked_ytrim_relu_p_kernel(
 
         scale_win = sb.tile([P, T], U8, name="scale_win", tag="scale_win", align_bytes=ALIGN)
         word_win = sb.tile([P, T], I32, name="word_win", align_bytes=ALIGN)
-        stage = sb.tile([P, 3 * H], F32, name="stage", align_bytes=ALIGN)
-        w1_second = sb.tile([P, 2, H], F32, name="w1_second", align_bytes=ALIGN)
-        w1_raw = [stage[:, H : 3 * H].rearrange("p (j c) -> p j c", j=2), w1_second[:]]
-        w2_raw = stage[:, 0 : PACK * N].rearrange("p (j n) -> p j n", j=PACK)
+        stage = sb.tile([P, PACK * (H + N) - SHARED], F32, name="stage", align_bytes=ALIGN)
+        w1_raw = stage[:, 0 : PACK * H].rearrange("p (j c) -> p j c", j=PACK)
+        w2_raw = stage[:, PACK * H - SHARED :].rearrange("p (j n) -> p j n", j=PACK)
         x_sc = sb.tile([P, S], U8, name="x_sc", align_bytes=ALIGN)
 
         nc.vector.memset(scale_win[:].bitcast(I32), 0)
@@ -53,14 +53,14 @@ def tile_picked_ytrim_relu_p_kernel(
 
         w1_rows = w1.rearrange("(p j) c -> p j c", j=PACK)
         w2_rows = w2.rearrange("(p j) n -> p j n", j=PACK)
-        nc.sync.dma_start(w1_raw[0], w1_rows[:, 0:2, :])
+        nc.sync.dma_start(w1_raw[:, 0:2, :], w1_rows[:, 0:2, :])
         nc.sync.dma_start(offs_sb[:], offs)
         nc.sync.dma_start(pos_sb[0][:], pos1)
         nc.sync.dma_start(scale_win[0:P:SPREAD, :].bitcast(I32), x_scales[0].bitcast(I32))
         nc.sync.dma_start(pos_sb[1][:], pos2)
-        nc.sync.dma_start(w1_raw[1], w1_rows[:, 2:4, :])
+        nc.sync.dma_start(w1_raw[:, 2:4, :], w1_rows[:, 2:4, :])
         nc.sync.dma_start(word_win[:], x_words[0].rearrange("p n t -> p (n t)").bitcast(I32))
-        nc.sync.dma_start(w2_raw[:, 0:2, :], w2_rows[:, 0:2, :])
+        nc.sync.dma_start(w2_raw[:, 2:4, :], w2_rows[:, 2:4, :])
         nc.sync.dma_start(pos_sb[2][:], pos3)
 
         sc_spread = sb.tile([P, S], U8, name="sc_spread", align_bytes=ALIGN)
@@ -72,11 +72,12 @@ def tile_picked_ytrim_relu_p_kernel(
         w1_q = sb.tile([P, H], U32, name="w1_q", tag="w1_q", align_bytes=ALIGN)
         w1_sc = sb.tile([P, H], U8, name="w1_sc", tag="w1_sc", align_bytes=ALIGN)
         w1_dst = w1_bf[:].rearrange("p (t m j) -> p m j t", t=PACK, j=PACK)
-        w1_src = [w1_raw[a].rearrange("p j (m t) -> p m j t", t=PACK) for a in range(2)]
-        nc.scalar.copy(w1_dst[:, :, 0:2, :], w1_src[0])
-        nc.sync.dma_start(w2_raw[:, 2:4, :], w2_rows[:, 2:4, :])
-        nc.scalar.copy(w1_dst[:, 0:SCALAR_DEALS, 2:4, :], w1_src[1][:, 0:SCALAR_DEALS])
-        nc.vector.tensor_copy(w1_dst[:, SCALAR_DEALS:P, 2:4, :], w1_src[1][:, SCALAR_DEALS:P])
+        w1_src = w1_raw.rearrange("p j (m t) -> p m j t", t=PACK)
+        tail = slice(VECTOR_DEALS, P)
+        for j in (0, 2):
+            nc.scalar.copy(w1_dst[:, tail, j : j + 2, :], w1_src[:, tail, j : j + 2, :])
+        nc.sync.dma_start(w2_raw[:, 0:2, :], w2_rows[:, 0:2, :])
+        nc.vector.tensor_copy(w1_dst[:, 0:VECTOR_DEALS], w1_src[:, 0:VECTOR_DEALS])
         nc.vector.quantize_mx(out=w1_q[:].bitcast(FP8X4), scales=w1_sc[:], in_=w1_bf[:])
 
         x_q = sb.tile([P, S], U32, name="x_q", tag="x_q", align_bytes=ALIGN)

@@ -23,7 +23,7 @@ PIECE = 128
 PIECES = S // PIECE
 HALF_V = V // 2
 RUN = 4
-SPREAD = 8
+SPREAD = P // 16
 VECTOR_DEALS = 72
 SHARED = 32
 ALIGN = 64
@@ -41,7 +41,7 @@ def tile_picked_ytrim_relu_p_kernel(
         offs_sb = lists.tile([P, S // LIST_ROWS], U16, name="offs_sb")
         pos_sb = [lists.tile([P, V // LIST_ROWS], U16, name="pos_sb%d" % d) for d in range(3)]
 
-        scale_win = sb.tile([P, T], U8, name="scale_win", tag="scale_win", align_bytes=ALIGN)
+        scale_win = sb.tile([P, T], U8, name="scale_win", align_bytes=ALIGN)
         word_win = sb.tile([P, T], I32, name="word_win", align_bytes=ALIGN)
         stage = sb.tile([P, PACK * (H + N) - SHARED], F32, name="stage", align_bytes=ALIGN)
         w1_raw = stage[:, 0 : PACK * H].rearrange("p (j c) -> p j c", j=PACK)
@@ -70,12 +70,11 @@ def tile_picked_ytrim_relu_p_kernel(
 
         w1_bf = sb.tile([P, H * PACK], BF16, name="w1_bf", align_bytes=ALIGN)
         w1_q = sb.tile([P, H], U32, name="w1_q", tag="w1_q", align_bytes=ALIGN)
-        w1_sc = sb.tile([P, H], U8, name="w1_sc", tag="w1_sc", align_bytes=ALIGN)
+        w1_sc = sb.tile([P, H], U8, name="w1_sc", align_bytes=ALIGN)
         w1_dst = w1_bf[:].rearrange("p (t m j) -> p m j t", t=PACK, j=PACK)
         w1_src = w1_raw.rearrange("p j (m t) -> p m j t", t=PACK)
-        tail = slice(VECTOR_DEALS, P)
         for j in (0, 2):
-            nc.scalar.copy(w1_dst[:, tail, j : j + 2, :], w1_src[:, tail, j : j + 2, :])
+            nc.scalar.copy(w1_dst[:, VECTOR_DEALS:P, j : j + 2, :], w1_src[:, VECTOR_DEALS:P, j : j + 2, :])
         nc.sync.dma_start(w2_raw[:, 0:2, :], w2_rows[:, 0:2, :])
         nc.vector.tensor_copy(w1_dst[:, 0:VECTOR_DEALS], w1_src[:, 0:VECTOR_DEALS])
         nc.vector.quantize_mx(out=w1_q[:].bitcast(FP8X4), scales=w1_sc[:], in_=w1_bf[:])
@@ -96,23 +95,29 @@ def tile_picked_ytrim_relu_p_kernel(
                 start=True, stop=True,
             )
 
+        def fetch_on_vector(dst, t, offsets):
+            nc.vector.tensor_copy(dst, h[t][:].indirect(offsets))
+
+        def fetch_on_scalar(dst, t, offsets):
+            nc.scalar.activation(dst, h[t][:].indirect(offsets), ACT.Copy)
+
         h = [sb.tile([P, S], F32, name="h%d" % t) for t in range(PACK)]
+        pairs = [psum.tile([P, 2, PIECE], F32, name="pair%d" % e, tag="bank%d" % (PIECES + e)) for e in range(2)]
         for a in range(PIECES):
             cols = slice(a * PIECE, (a + 1) * PIECE)
             piece = psum.tile([P, PIECE], F32, name="piece%d" % a, tag="bank%d" % a)
             first_product(piece[:], 0, cols)
             nc.scalar.copy(h[0][:, cols], piece[:])
+            first_product(pairs[a // 2][:, a % 2, :], 1, cols)
             if a % 2 == 1:
-                cols = slice((a - 1) * PIECE, (a + 1) * PIECE)
-                pair = psum.tile([P, 2 * PIECE], F32, name="pair%d" % a, tag="bank%d" % (4 + a // 2))
-                first_product(pair[:], 1, cols)
-                nc.scalar.copy(h[1][:, cols], pair[:])
-        g01 = [sb.tile([P, 2, V], BF16, name="g%d" % d, align_bytes=ALIGN) for d in range(2)]
-        nc.scalar.activation(g01[1][:, 0, :], h[0][:].indirect(pos_sb[1][:]), ACT.Copy)
+                nc.scalar.copy(h[1][:, (a - 1) * PIECE : (a + 1) * PIECE], pairs[a // 2][:].rearrange("p a c -> p (a c)"))
+        g0_early = sb.tile([P, 2, V], BF16, name="g0_early", align_bytes=ALIGN)
+        g1_early = sb.tile([P, 2, V], BF16, name="g1_early", align_bytes=ALIGN)
+        fetch_on_scalar(g1_early[:, 0, :], 0, pos_sb[1][:])
         for t in range(2, PACK):
-            late = psum.tile([P, S], F32, name="late%d" % t, tag="bank%d" % (4 + t))
-            first_product(late[:], t, slice(0, S))
-            nc.scalar.copy(h[t][:], late[:])
+            whole = psum.tile([P, S], F32, name="whole%d" % t, tag="bank%d" % (PIECES + t))
+            first_product(whole[:], t, slice(0, S))
+            nc.scalar.copy(h[t][:], whole[:])
 
         w2_bf = sb.tile([P, N * PACK], BF16, name="w2_bf", align_bytes=ALIGN)
         w2_dst = w2_bf[:].rearrange("p (b m j) -> p b m j", b=2, j=PACK)
@@ -122,38 +127,31 @@ def tile_picked_ytrim_relu_p_kernel(
 
         halves = [slice(u * HALF_V, (u + 1) * HALF_V) for u in range(2)]
         entries = [slice(half.start // LIST_ROWS, half.stop // LIST_ROWS) for half in halves]
-        w2_q = [None, None]
         w2_sc = [sb.tile([P, P], U8, name="w2_sc%d" % b, align_bytes=ALIGN) for b in range(2)]
 
         def quantise_w2(b, tag):
-            w2_q[b] = sb.tile([P, P], U32, name="w2_q%d" % b, tag=tag, align_bytes=ALIGN)
+            codes = sb.tile([P, P], U32, name="w2_q%d" % b, tag=tag, align_bytes=ALIGN)
             nc.vector.quantize_mx(
-                out=w2_q[b][:].bitcast(FP8X4), scales=w2_sc[b][:], in_=w2_bf[:, b * P * PACK : (b + 1) * P * PACK]
+                out=codes[:].bitcast(FP8X4), scales=w2_sc[b][:], in_=w2_bf[:, b * P * PACK : (b + 1) * P * PACK]
             )
+            return codes
 
-        quantise_w2(0, "w2_q0")
+        w2_q = [quantise_w2(0, "w2_q0")]
 
         shelf = sb.tile([P, 14, HALF_V], BF16, name="shelf", align_bytes=ALIGN)
         g2_first = shelf[:, 2:6, :]
         hi = sb.tile([P, PACK, V], BF16, name="hi", align_bytes=ALIGN)
         lo = sb.tile([P, PACK, V], BF16, name="lo", align_bytes=ALIGN)
-        capped_first = sb.tile([P, PACK, HALF_V], BF16, name="capped_first", align_bytes=ALIGN)
-        capped = [capped_first[:], shelf[:, 1:5, :]]
+        capped_first = sb.tile([P, PACK, HALF_V], BF16, name="capped_first", tag="capped_first", align_bytes=ALIGN)
+        capped_second = shelf[:, 1:5, :]
         g0_late = shelf[:].rearrange("p (t a) v -> p t (a v)", t=2)[:, :, 0:V]
         g1_late = sb.tile([P, 2, V], BF16, name="g1_late", tag="w1_q", align_bytes=ALIGN)
-        g2_mid = sb.tile([P, 2, HALF_V], BF16, name="g2_mid", tag="x_q", align_bytes=ALIGN)
-        g2_last = sb.tile([P, HALF_V], BF16, name="g2_last", tag="w1_sc", align_bytes=ALIGN)
+        g2_second = sb.tile([P, PACK - 1, HALF_V], BF16, name="g2_second", tag="x_q", align_bytes=ALIGN)
 
-        def fetch_on_vector(dst, t, offsets):
-            nc.vector.tensor_copy(dst, h[t][:].indirect(offsets))
-
-        def fetch_on_scalar(dst, t, offsets):
-            nc.scalar.activation(dst, h[t][:].indirect(offsets), ACT.Copy)
-
-        fetch_on_vector(g01[0][:, 0, :], 0, pos_sb[0][:])
+        fetch_on_vector(g0_early[:, 0, :], 0, pos_sb[0][:])
         fetch_on_vector(shelf[:, 2:7:4, :], 0, pos_sb[2][:])
-        for d in range(2):
-            fetch_on_vector(g01[d][:, 1, :], 1, pos_sb[d][:])
+        fetch_on_vector(g0_early[:, 1, :], 1, pos_sb[0][:])
+        fetch_on_vector(g1_early[:, 1, :], 1, pos_sb[1][:])
         fetch_on_vector(g2_first[:, 1, :], 1, pos_sb[2][:, entries[0]])
         fetch_on_vector(g0_late[:, 0, :], 2, pos_sb[0][:])
         fetch_on_scalar(g1_late[:, 0, :], 2, pos_sb[1][:])
@@ -161,9 +159,8 @@ def tile_picked_ytrim_relu_p_kernel(
         fetch_on_scalar(g1_late[:, 1, :], 3, pos_sb[1][:])
         for t in range(2, PACK):
             fetch_on_scalar(g2_first[:, t, :], t, pos_sb[2][:, entries[0]])
-        for t in range(1, 3):
-            fetch_on_scalar(g2_mid[:, t - 1, :], t, pos_sb[2][:, entries[1]])
-        fetch_on_scalar(g2_last[:], 3, pos_sb[2][:, entries[1]])
+        for t in range(1, PACK):
+            fetch_on_scalar(g2_second[:, t - 1, :], t, pos_sb[2][:, entries[1]])
 
         z_first = sb.tile([P, PACK, HALF_V], BF16, name="z_first", align_bytes=ALIGN)
         z_bf = [sb.tile([P, HALF_V * PACK], BF16, name="z_bf%d" % u, align_bytes=ALIGN) for u in range(2)]
@@ -176,35 +173,29 @@ def tile_picked_ytrim_relu_p_kernel(
         def in_runs(ap):
             return ap.rearrange("p t (c r) -> p c t r", r=RUN)
 
-        for tiles, g0, g1 in ((slice(0, 2), g01[0][:], g01[1][:]), (slice(2, 4), g0_late, g1_late[:])):
+        for tiles, g0, g1 in ((slice(0, 2), g0_early[:], g1_early[:]), (slice(2, PACK), g0_late, g1_late[:])):
             nc.vector.tensor_tensor(hi[:, tiles, :], g0, g1, ALU.max)
             nc.vector.tensor_tensor(lo[:, tiles, :], g0, g1, ALU.min)
-        nc.vector.tensor_tensor(capped[0], hi[:, :, halves[0]], g2_first, ALU.min)
-        nc.vector.tensor_tensor(capped[1][:, 0, :], hi[:, 0, halves[1]], shelf[:, 6, :], ALU.min)
-        nc.vector.tensor_tensor(z_first[:], capped[0], lo[:, :, halves[0]], ALU.max)
+        nc.vector.tensor_tensor(capped_first[:], hi[:, :, halves[0]], g2_first, ALU.min)
+        nc.vector.tensor_tensor(capped_second[:, 0, :], hi[:, 0, halves[1]], shelf[:, 6, :], ALU.min)
+        nc.vector.tensor_tensor(z_first[:], capped_first[:], lo[:, :, halves[0]], ALU.max)
         nc.scalar.copy(woven(z_bf[0][:]), in_runs(z_first[:]))
-        nc.vector.tensor_tensor(capped[1][:, 1:3, :], hi[:, 1:3, halves[1]], g2_mid[:], ALU.min)
-        nc.vector.tensor_tensor(capped[1][:, 3, :], hi[:, 3, halves[1]], g2_last[:], ALU.min)
-        quantise_w2(1, "x_q")
-        nc.vector.tensor_tensor(woven(z_bf[1][:]), in_runs(capped[1]), in_runs(lo[:, :, halves[1]]), ALU.max)
+        nc.vector.tensor_tensor(capped_second[:, 1:PACK, :], hi[:, 1:PACK, halves[1]], g2_second[:], ALU.min)
+        w2_q.append(quantise_w2(1, "capped_first"))
+        nc.vector.tensor_tensor(woven(z_bf[1][:]), in_runs(capped_second), in_runs(lo[:, :, halves[1]]), ALU.max)
         for u in range(2):
             nc.vector.quantize_mx(out=z_q[u][:].bitcast(FP8X4), scales=z_sc[u][:], in_=z_bf[u][:])
 
-        def second_product(acc, u, b):
-            nc.tensor.matmul_mx(
-                out=acc, lhsT=w2_q[b][:].bitcast(FP8X4), lhsT_scale=w2_sc[b][:],
-                rhs=z_q[u][:].bitcast(FP8X4), rhs_scale=z_sc[u][:], start=True, stop=True,
-            )
-
         res = sb.tile([P, 2, V], F32, name="res")
-        out_first = psum.tile([P, 2, HALF_V], F32, name="out_first", tag="bank0")
-        for b in range(2):
-            second_product(out_first[:, b, :], 0, b)
-        nc.scalar.activation(res[:, :, halves[0]], out_first[:], ACT.Relu)
-        out_upper = psum.tile([P, HALF_V], F32, name="out_upper", tag="bank1")
-        second_product(out_upper[:], 1, 0)
-        nc.vector.tensor_scalar_max(res[:, 0, halves[1]], out_upper[:], 0.0)
-        out_lower = psum.tile([P, HALF_V], F32, name="out_lower", tag="bank2")
-        second_product(out_lower[:], 1, 1)
-        nc.scalar.activation(res[:, 1, halves[1]], out_lower[:], ACT.Relu)
+        for u in range(2):
+            for b in range(2):
+                acc = psum.tile([P, HALF_V], F32, name="acc%d%d" % (u, b), tag="bank%d" % (2 * u + b))
+                nc.tensor.matmul_mx(
+                    out=acc[:], lhsT=w2_q[b][:].bitcast(FP8X4), lhsT_scale=w2_sc[b][:],
+                    rhs=z_q[u][:].bitcast(FP8X4), rhs_scale=z_sc[u][:], start=True, stop=True,
+                )
+                if b == 0:
+                    nc.vector.tensor_scalar_max(res[:, b, halves[u]], acc[:], 0.0)
+                else:
+                    nc.scalar.activation(res[:, b, halves[u]], acc[:], ACT.Relu)
         nc.sync.dma_start(out.rearrange("(p b) v -> p b v", b=2), res[:])

@@ -73,9 +73,11 @@ def tile_picked_ytrim_relu_p_kernel(
         w1_sc = sb.tile([P, H], U8, name="w1_sc", align_bytes=ALIGN)
         w1_dst = w1_bf[:].rearrange("p (t m j) -> p m j t", t=PACK, j=PACK)
         w1_src = w1_raw.rearrange("p j (m t) -> p m j t", t=PACK)
-        for j in (0, 2):
-            nc.scalar.copy(w1_dst[:, VECTOR_DEALS:P, j : j + 2, :], w1_src[:, VECTOR_DEALS:P, j : j + 2, :])
+        strip = P - SHARED // PACK
+        nc.scalar.copy(w1_dst[:, VECTOR_DEALS:P, 0:2, :], w1_src[:, VECTOR_DEALS:P, 0:2, :])
+        nc.vector.tensor_copy(w1_dst[:, strip:P, 2:4, :], w1_src[:, strip:P, 2:4, :])
         nc.sync.dma_start(w2_raw[:, 0:2, :], w2_rows[:, 0:2, :])
+        nc.scalar.copy(w1_dst[:, VECTOR_DEALS:strip, 2:4, :], w1_src[:, VECTOR_DEALS:strip, 2:4, :])
         nc.vector.tensor_copy(w1_dst[:, 0:VECTOR_DEALS], w1_src[:, 0:VECTOR_DEALS])
         nc.vector.quantize_mx(out=w1_q[:].bitcast(FP8X4), scales=w1_sc[:], in_=w1_bf[:])
 

@@ -60,7 +60,7 @@ def tile_picked_ytrim_relu_p_kernel(
         nc.sync.dma_start(pos_sb[1][:], pos2)
         nc.sync.dma_start(w1_raw[:, 2:4, :], w1_rows[:, 2:4, :])
         nc.sync.dma_start(word_win[:], x_words[0].rearrange("p n t -> p (n t)").bitcast(I32))
-        nc.sync.dma_start(w2_raw[:, 2:4, :], w2_rows[:, 2:4, :])
+        nc.sync.dma_start(w2_raw[:, 3, :], w2_rows[:, 3, :])
         nc.sync.dma_start(pos_sb[2][:], pos3)
 
         sc_spread = sb.tile([P, S], U8, name="sc_spread", align_bytes=ALIGN)
@@ -76,7 +76,7 @@ def tile_picked_ytrim_relu_p_kernel(
         strip = P - SHARED // PACK
         nc.scalar.copy(w1_dst[:, VECTOR_DEALS:P, 0:2, :], w1_src[:, VECTOR_DEALS:P, 0:2, :])
         nc.vector.tensor_copy(w1_dst[:, strip:P, 2:4, :], w1_src[:, strip:P, 2:4, :])
-        nc.sync.dma_start(w2_raw[:, 0:2, :], w2_rows[:, 0:2, :])
+        nc.sync.dma_start(w2_raw[:, 0:3, :], w2_rows[:, 0:3, :])
         nc.scalar.copy(w1_dst[:, VECTOR_DEALS:strip, 2:4, :], w1_src[:, VECTOR_DEALS:strip, 2:4, :])
         nc.vector.tensor_copy(w1_dst[:, 0:VECTOR_DEALS], w1_src[:, 0:VECTOR_DEALS])
         nc.vector.quantize_mx(out=w1_q[:].bitcast(FP8X4), scales=w1_sc[:], in_=w1_bf[:])

@@ -25,7 +25,8 @@ HALF_V = V // 2
 RUN = 4
 SPREAD = P // 16
 VECTOR_DEALS = 72
-SHARED = 32
+SHARED = 64
+BURST = 256
 ALIGN = 64
 
 
@@ -41,12 +42,12 @@ def tile_picked_ytrim_relu_p_kernel(
         offs_sb = lists.tile([P, S // LIST_ROWS], U16, name="offs_sb")
         pos_sb = [lists.tile([P, V // LIST_ROWS], U16, name="pos_sb%d" % d) for d in range(3)]
 
-        scale_win = sb.tile([P, T], U8, name="scale_win", align_bytes=ALIGN)
-        word_win = sb.tile([P, T], I32, name="word_win", align_bytes=ALIGN)
-        stage = sb.tile([P, PACK * (H + N) - SHARED], F32, name="stage", align_bytes=ALIGN)
+        scale_win = sb.tile([P, T], U8, name="scale_win", align_bytes=BURST)
+        word_win = sb.tile([P, T], I32, name="word_win", align_bytes=BURST)
+        stage = sb.tile([P, PACK * (H + N) - SHARED], F32, name="stage", align_bytes=BURST)
         w1_raw = stage[:, 0 : PACK * H].rearrange("p (j c) -> p j c", j=PACK)
         w2_raw = stage[:, PACK * H - SHARED :].rearrange("p (j n) -> p j n", j=PACK)
-        x_sc = sb.tile([P, S], U8, name="x_sc", align_bytes=ALIGN)
+        x_sc = sb.tile([P, S], U8, name="x_sc", align_bytes=BURST)
 
         nc.vector.memset(scale_win[:].bitcast(I32), 0)
         nc.vector.memset(x_sc[:].bitcast(I32), 0)
@@ -63,7 +64,7 @@ def tile_picked_ytrim_relu_p_kernel(
         nc.sync.dma_start(w2_raw[:, 3, :], w2_rows[:, 3, :])
         nc.sync.dma_start(pos_sb[2][:], pos3)
 
-        sc_spread = sb.tile([P, S], U8, name="sc_spread", align_bytes=ALIGN)
+        sc_spread = sb.tile([P, S], U8, name="sc_spread", align_bytes=BURST)
         nc.vector.tensor_copy(sc_spread[:], scale_win[:].indirect(offs_sb[:]))
         for r in range(4):
             nc.sync.dma_start(x_sc[r:P:QUADRANT, :].bitcast(I32), sc_spread[r * SPREAD : P : QUADRANT, :].bitcast(I32))
@@ -188,7 +189,7 @@ def tile_picked_ytrim_relu_p_kernel(
         for u in range(2):
             nc.vector.quantize_mx(out=z_q[u][:].bitcast(FP8X4), scales=z_sc[u][:], in_=z_bf[u][:])
 
-        res = sb.tile([P, 2, V], F32, name="res")
+        res = sb.tile([P, 2, V], F32, name="res", align_bytes=BURST)
         for u in range(2):
             for b in range(2):
                 acc = psum.tile([P, HALF_V], F32, name="acc%d%d" % (u, b), tag="bank%d" % (2 * u + b))

from contextlib import ExitStack

import concourse.mybir as mybir

K, T, S, V, H, N = 512, 2048, 512, 256, 512, 256
FLOPS = 2 * K * H * S + 2 * H * N * V

F32 = mybir.dt.float32
BF16 = mybir.dt.bfloat16
I32 = mybir.dt.int32
U32 = mybir.dt.uint32
U16 = mybir.dt.uint16
U8 = mybir.dt.uint8
FP8X4 = mybir.dt.float8_e4m3fn_x4
ALU = mybir.AluOpType
ACT = mybir.ActivationFunctionType

P = 128
PACK = 4
LIST_ROWS = 16
QUADRANT = 32
PIECE = 128
PIECES = S // PIECE
HALF_V = V // 2
RUN = 4
SPREAD = P // 16
VECTOR_DEALS = 72
SHARED = 64
BURST = 256
ALIGN = 64


def tile_picked_ytrim_relu_p_kernel(
    tc, x_words, x_scales, w1, w2, offs, pos1, pos2, pos3, out
):
    nc = tc.nc
    with ExitStack() as ctx:
        lists = ctx.enter_context(tc.tile_pool(name="lists", bufs=1))
        sb = ctx.enter_context(tc.tile_pool(name="sb", bufs=1))
        psum = ctx.enter_context(tc.psum_pool(name="psum", bufs=1))

        offs_sb = lists.tile([P, S // LIST_ROWS], U16, name="offs_sb")
        pos_sb = [lists.tile([P, V // LIST_ROWS], U16, name="pos_sb%d" % d) for d in range(3)]

        scale_win = sb.tile([P, T], U8, name="scale_win", align_bytes=BURST)
        word_win = sb.tile([P, T], I32, name="word_win", align_bytes=BURST)
        stage = sb.tile([P, PACK * (H + N) - SHARED], F32, name="stage", align_bytes=BURST)
        w1_raw = stage[:, 0 : PACK * H].rearrange("p (j c) -> p j c", j=PACK)
        w2_raw = stage[:, PACK * H - SHARED :].rearrange("p (j n) -> p j n", j=PACK)
        x_sc = sb.tile([P, S], U8, name="x_sc", align_bytes=BURST)

        nc.vector.memset(scale_win[:].bitcast(I32), 0)
        nc.vector.memset(x_sc[:].bitcast(I32), 0)

        w1_rows = w1.rearrange("(p j) c -> p j c", j=PACK)
        w2_rows = w2.rearrange("(p j) n -> p j n", j=PACK)
        nc.sync.dma_start(w1_raw[:, 0:2, :], w1_rows[:, 0:2, :])
        nc.sync.dma_start(offs_sb[:], offs)
        nc.sync.dma_start(pos_sb[0][:], pos1)
        nc.sync.dma_start(scale_win[0:P:SPREAD, :].bitcast(I32), x_scales[0].bitcast(I32))
        nc.sync.dma_start(pos_sb[1][:], pos2)
        nc.sync.dma_start(w1_raw[:, 2:4, :], w1_rows[:, 2:4, :])
        nc.sync.dma_start(word_win[:], x_words[0].rearrange("p n t -> p (n t)").bitcast(I32))
        nc.sync.dma_start(w2_raw[:, 3, :], w2_rows[:, 3, :])
        nc.sync.dma_start(pos_sb[2][:], pos3)

        sc_spread = sb.tile([P, S], U8, name="sc_spread", align_bytes=BURST)
        nc.vector.tensor_copy(sc_spread[:], scale_win[:].indirect(offs_sb[:]))
        for r in range(4):
            nc.sync.dma_start(x_sc[r:P:QUADRANT, :].bitcast(I32), sc_spread[r * SPREAD : P : QUADRANT, :].bitcast(I32))

        w1_bf = sb.tile([P, H * PACK], BF16, name="w1_bf", align_bytes=ALIGN)
        w1_q = sb.tile([P, H], U32, name="w1_q", tag="w1_q", align_bytes=ALIGN)
        w1_sc = sb.tile([P, H], U8, name="w1_sc", align_bytes=ALIGN)
        w1_dst = w1_bf[:].rearrange("p (t m j) -> p m j t", t=PACK, j=PACK)
        w1_src = w1_raw.rearrange("p j (m t) -> p m j t", t=PACK)
        strip = P - SHARED // PACK
        nc.scalar.copy(w1_dst[:, VECTOR_DEALS:P, 0:2, :], w1_src[:, VECTOR_DEALS:P, 0:2, :])
        nc.vector.tensor_copy(w1_dst[:, strip:P, 2:4, :], w1_src[:, strip:P, 2:4, :])
        nc.sync.dma_start(w2_raw[:, 0:3, :], w2_rows[:, 0:3, :])
        nc.scalar.copy(w1_dst[:, VECTOR_DEALS:strip, 2:4, :], w1_src[:, VECTOR_DEALS:strip, 2:4, :])
        nc.vector.tensor_copy(w1_dst[:, 0:VECTOR_DEALS], w1_src[:, 0:VECTOR_DEALS])
        nc.vector.quantize_mx(out=w1_q[:].bitcast(FP8X4), scales=w1_sc[:], in_=w1_bf[:])

        x_q = sb.tile([P, S], U32, name="x_q", tag="x_q", align_bytes=ALIGN)
        list_cols = PIECE // LIST_ROWS
        for a in range(PIECES):
            nc.vector.tensor_copy(
                x_q[:, a * PIECE : (a + 1) * PIECE],
                word_win[:].bitcast(U32).indirect(offs_sb[:, a * list_cols : (a + 1) * list_cols]),
            )

        def first_product(acc, t, cols):
            group = slice(t * P, (t + 1) * P)
            nc.tensor.matmul_mx(
                out=acc, lhsT=w1_q[:, group].bitcast(FP8X4), lhsT_scale=w1_sc[:, group],
                rhs=x_q[:, cols].bitcast(FP8X4), rhs_scale=x_sc[:, cols],
                start=True, stop=True,
            )

        def fetch_on_vector(dst, t, offsets):
            nc.vector.tensor_copy(dst, h[t][:].indirect(offsets))

        def fetch_on_scalar(dst, t, offsets):
            nc.scalar.activation(dst, h[t][:].indirect(offsets), ACT.Copy)

        h = [sb.tile([P, S], F32, name="h%d" % t) for t in range(PACK)]
        pairs = [psum.tile([P, 2, PIECE], F32, name="pair%d" % e, tag="bank%d" % (PIECES + e)) for e in range(2)]
        for a in range(PIECES):
            cols = slice(a * PIECE, (a + 1) * PIECE)
            piece = psum.tile([P, PIECE], F32, name="piece%d" % a, tag="bank%d" % a)
            first_product(piece[:], 0, cols)
            nc.scalar.copy(h[0][:, cols], piece[:])
            first_product(pairs[a // 2][:, a % 2, :], 1, cols)
            if a % 2 == 1:
                nc.scalar.copy(h[1][:, (a - 1) * PIECE : (a + 1) * PIECE], pairs[a // 2][:].rearrange("p a c -> p (a c)"))
        g0_early = sb.tile([P, 2, V], BF16, name="g0_early", align_bytes=ALIGN)
        g1_early = sb.tile([P, 2, V], BF16, name="g1_early", align_bytes=ALIGN)
        fetch_on_scalar(g1_early[:, 0, :], 0, pos_sb[1][:])
        for t in range(2, PACK):
            whole = psum.tile([P, S], F32, name="whole%d" % t, tag="bank%d" % (PIECES + t))
            first_product(whole[:], t, slice(0, S))
            nc.scalar.copy(h[t][:], whole[:])

        w2_bf = sb.tile([P, N * PACK], BF16, name="w2_bf", align_bytes=ALIGN)
        w2_dst = w2_bf[:].rearrange("p (b m j) -> p b m j", b=2, j=PACK)
        w2_src = w2_raw.rearrange("p j (m b) -> p b m j", b=2)
        for b in range(2):
            nc.vector.tensor_copy(w2_dst[:, b], w2_src[:, b])

        halves = [slice(u * HALF_V, (u + 1) * HALF_V) for u in range(2)]
        entries = [slice(half.start // LIST_ROWS, half.stop // LIST_ROWS) for half in halves]
        w2_sc = [sb.tile([P, P], U8, name="w2_sc%d" % b, align_bytes=ALIGN) for b in range(2)]

        def quantise_w2(b, tag):
            codes = sb.tile([P, P], U32, name="w2_q%d" % b, tag=tag, align_bytes=ALIGN)
            nc.vector.quantize_mx(
                out=codes[:].bitcast(FP8X4), scales=w2_sc[b][:], in_=w2_bf[:, b * P * PACK : (b + 1) * P * PACK]
            )
            return codes

        w2_q = [quantise_w2(0, "w2_q0")]

        shelf = sb.tile([P, 14, HALF_V], BF16, name="shelf", align_bytes=ALIGN)
        g2_first = shelf[:, 2:6, :]
        hi = sb.tile([P, PACK, V], BF16, name="hi", align_bytes=ALIGN)
        lo = sb.tile([P, PACK, V], BF16, name="lo", align_bytes=ALIGN)
        capped_first = sb.tile([P, PACK, HALF_V], BF16, name="capped_first", tag="capped_first", align_bytes=ALIGN)
        capped_second = shelf[:, 1:5, :]
        g0_late = shelf[:].rearrange("p (t a) v -> p t (a v)", t=2)[:, :, 0:V]
        g1_late = sb.tile([P, 2, V], BF16, name="g1_late", tag="w1_q", align_bytes=ALIGN)
        g2_second = sb.tile([P, PACK - 1, HALF_V], BF16, name="g2_second", tag="x_q", align_bytes=ALIGN)

        fetch_on_vector(g0_early[:, 0, :], 0, pos_sb[0][:])
        fetch_on_vector(shelf[:, 2:7:4, :], 0, pos_sb[2][:])
        fetch_on_vector(g0_early[:, 1, :], 1, pos_sb[0][:])
        fetch_on_vector(g1_early[:, 1, :], 1, pos_sb[1][:])
        fetch_on_vector(g2_first[:, 1, :], 1, pos_sb[2][:, entries[0]])
        fetch_on_vector(g0_late[:, 0, :], 2, pos_sb[0][:])
        fetch_on_scalar(g1_late[:, 0, :], 2, pos_sb[1][:])
        fetch_on_scalar(g0_late[:, 1, :], 3, pos_sb[0][:])
        fetch_on_scalar(g1_late[:, 1, :], 3, pos_sb[1][:])
        for t in range(2, PACK):
            fetch_on_scalar(g2_first[:, t, :], t, pos_sb[2][:, entries[0]])
        for t in range(1, PACK):
            fetch_on_scalar(g2_second[:, t - 1, :], t, pos_sb[2][:, entries[1]])

        z_first = sb.tile([P, PACK, HALF_V], BF16, name="z_first", align_bytes=ALIGN)
        z_bf = [sb.tile([P, HALF_V * PACK], BF16, name="z_bf%d" % u, align_bytes=ALIGN) for u in range(2)]
        z_q = [sb.tile([P, HALF_V], U32, name="z_q%d" % u, align_bytes=ALIGN) for u in range(2)]
        z_sc = [sb.tile([P, HALF_V], U8, name="z_sc%d" % u, align_bytes=ALIGN) for u in range(2)]

        def woven(ap):
            return ap.rearrange("p (c r t) -> p c t r", r=RUN, t=PACK)

        def in_runs(ap):
            return ap.rearrange("p t (c r) -> p c t r", r=RUN)

        for tiles, g0, g1 in ((slice(0, 2), g0_early[:], g1_early[:]), (slice(2, PACK), g0_late, g1_late[:])):
            nc.vector.tensor_tensor(hi[:, tiles, :], g0, g1, ALU.max)
            nc.vector.tensor_tensor(lo[:, tiles, :], g0, g1, ALU.min)
        nc.vector.tensor_tensor(capped_first[:], hi[:, :, halves[0]], g2_first, ALU.min)
        nc.vector.tensor_tensor(capped_second[:, 0, :], hi[:, 0, halves[1]], shelf[:, 6, :], ALU.min)
        nc.vector.tensor_tensor(z_first[:], capped_first[:], lo[:, :, halves[0]], ALU.max)
        nc.scalar.copy(woven(z_bf[0][:]), in_runs(z_first[:]))
        nc.vector.tensor_tensor(capped_second[:, 1:PACK, :], hi[:, 1:PACK, halves[1]], g2_second[:], ALU.min)
        w2_q.append(quantise_w2(1, "capped_first"))
        nc.vector.tensor_tensor(woven(z_bf[1][:]), in_runs(capped_second), in_runs(lo[:, :, halves[1]]), ALU.max)
        for u in range(2):
            nc.vector.quantize_mx(out=z_q[u][:].bitcast(FP8X4), scales=z_sc[u][:], in_=z_bf[u][:])

        res = sb.tile([P, 2, V], F32, name="res", align_bytes=BURST)
        for u in range(2):
            for b in range(2):
                acc = psum.tile([P, HALF_V], F32, name="acc%d%d" % (u, b), tag="bank%d" % (2 * u + b))
                nc.tensor.matmul_mx(
                    out=acc[:], lhsT=w2_q[b][:].bitcast(FP8X4), lhsT_scale=w2_sc[b][:],
                    rhs=z_q[u][:].bitcast(FP8X4), rhs_scale=z_sc[u][:], start=True, stop=True,
                )
                if b == 0:
                    nc.vector.tensor_scalar_max(res[:, b, halves[u]], acc[:], 0.0)
                else:
                    nc.scalar.activation(res[:, b, halves[u]], acc[:], ACT.Relu)
        nc.sync.dma_start(out.rearrange("(p b) v -> p b v", b=2), res[:])
